import numpy as np, ml_dtypes
CORES = [66,74,82,90,194,202,210,218]
N = 8
import mx_ref
BF = ml_dtypes.bfloat16
def gentries(a):
    return np.ascontiguousarray(a.reshape(8, 16, -1).transpose(0, 2, 1)).reshape(8, -1)
def gtable(e):
    e = np.asarray(e); return np.ascontiguousarray(e.reshape(8, -1, 16).transpose(0, 2, 1)).reshape(128, -1).astype(np.int32)
def gcols(t, e):
    v = np.concatenate([t.reshape(8, 16, -1, 4), np.zeros((8, 16, 1, 4), BF)], axis=2)
    return np.ascontiguousarray(np.stack([v[g][:, e[g]] for g in range(8)])).reshape(128, -1)
def tile(rs):
    return np.stack(rs, axis=2).reshape(128, -1).astype(BF)
def pick(q, e):
    c = np.concatenate([q[0].reshape(128, -1, 4), np.zeros((128, 1, 4), np.uint8)], axis=1); s = np.concatenate([q[1], np.ones((16, 1), np.uint8)], axis=1)
    return (np.ascontiguousarray(c[:, e].reshape(128, -1)), np.ascontiguousarray(s[:, e]))
def join(*qs):
    return (np.concatenate([q[0] for q in qs], axis=1), np.concatenate([q[1] for q in qs], axis=1))
def put(q, e, v):
    c, s = q[0].reshape(128, -1, 4).copy(), q[1].copy(); c[:, e] = v[0].reshape(128, -1, 4); s[:, e] = v[1]
    return (c.reshape(128, -1), s)
def pk(c, s):
    return (np.ascontiguousarray(c), mx_ref.live(s))
def emit(q):
    return q[0], q[1]
def packed(v, rng):
    q = [mx_ref.quantize(np.ascontiguousarray(v[r])) for r in range(N)]
    return np.stack([a for a, b in q]), np.stack([mx_ref.plane(b, rng) for a, b in q])
def values_of_codes():
    e, c = np.zeros((128, 128, 4), np.float32), np.zeros((128, 2, 4), np.uint8)
    e[np.arange(128), np.arange(128), 0] = 1
    c[:127, :, 0] = np.arange(256).reshape(2, 128).T[:127]
    return mx_ref.matmul(mx_ref.quantize(e.reshape(128, 512).astype(BF)), (c.reshape(128, 8), np.full((16, 2), 127, np.uint8))).T.reshape(-1).astype(np.float64)
CODE_VALUE, SCALE_VALUE = values_of_codes(), 2.0 ** (np.arange(256) - 127.0)
def decode(q):
    return (CODE_VALUE[q[0]].reshape(16, 8, -1, 4) * SCALE_VALUE[q[1]][:, None, :, None] + 0.0).reshape(128, -1).astype(np.float32)
def f(rng, *shape):
    return mx_ref.flush((rng.standard_normal(shape, dtype=np.float32) * np.exp2(rng.integers(-2, 3, shape[:-1] + (1,)))).astype(BF))
def wide(rng, *shape, cols=0):
    v = rng.standard_normal(shape, dtype=np.float32) * np.exp2(rng.integers(-12, 13, shape)).astype(np.float32)
    if cols: v *= np.repeat(np.exp2(rng.integers(-cols, cols + 1, shape[:-2] + (1, shape[-1] // 4))) * (rng.random(shape[:-2] + (1, shape[-1] // 4)) > 0.0625), 4, axis=-1).astype(np.float32)
    return mx_ref.flush(v.astype(BF))
C, HALF = 288, 144
MASK = [4, 1, 2]
def numbers_of(rng):
    return {"x": np.array(f(rng, N, 128, 4 * C)), "u": np.array(f(rng, N, 128, 512)), "v": np.array(f(rng, N, 128, 512))}
def orders(rng):
    e = np.tile(np.arange(C), (N, 8, 1))
    k = [rng.permuted(e, axis=2) for i in range(4)]
    t = np.zeros((N, 8, C), np.int64)
    np.put_along_axis(t, k[3], np.ascontiguousarray(k[3].reshape(N, 8, HALF, 2)[:, :, :, ::-1]).reshape(N, 8, C), axis=2)
    return k[:3] + [t]
def stored(k):
    return {n: np.stack([gtable(a[r]) for r in range(N)]) for n, a in zip(("lg", "pb", "fd", "ex"), k)}
def lists(rng):
    return stored(orders(rng))
def layers(rng):
    return np.array(f(rng, N, 128, 2048)).reshape(N, 8, 16, 4, 8, 16, 4)
def weights(rng, w):
    c, p = packed(np.ascontiguousarray(w).reshape(N, 128, 2048), rng)
    return {"wc": c, "ws": p}
def setup_inputs(rng):
    return {**numbers_of(rng), **lists(rng), **weights(rng, layers(rng))}
def setup_inputs_ties(rng):
    d = numbers_of(rng)
    o = rng.permutation(N)
    k = rng.integers(-1, 2, (N, 8, 4, C)).astype(np.float32)
    k[o[1]] = 1
    k[o[2]] = -1
    x = d["x"].reshape(N, 8, 16, C, 4)
    x[:, :, :4] = 0
    x[:, :, :4, :, 0] = k.astype(BF)
    u = d["u"].reshape(N, 8, 16, 8, 16, 4)
    u[:, :, :, :, :4] = 0
    for g in range(8):
        for j in range(4): u[:, g, j, g, j, 0] = 1.0
    u[o[0], :, :, :, :4] = 0
    w = layers(rng)
    w[:, :, :, :, :, :4] = 0
    return {"x": x.reshape(N, 128, 4 * C), "u": u.reshape(N, 128, 512), "v": d["v"], **lists(rng), **weights(rng, w)}
def setup_inputs_near(rng):
    d = numbers_of(rng)
    o = rng.permutation(N)
    k = np.ones(N, np.float32)
    k[o[:N // 2]] = 2.0 ** -30
    s = rng.integers(-1, 2, (N, 8, 4, C)) * np.where(k < 1, 2 * k, k)[:, None, None, None]
    x = d["x"].astype(np.float32).reshape(N, 8, 16, C, 4)
    x[:, :, :8] = 0
    x[:, :, 0:8:2, :, 0] = 1.125 * s
    x[:, :, 1:8:2, :, 0] = -1.25 * s
    for r in range(N):
        at_ = [0, C - 1, int(rng.integers(C)), int(rng.integers(C))]
        for g, c in zip(rng.permutation(8)[:4], at_): x[r, g, 2 * rng.integers(4), c, 0] = 2.0 ** 30 * rng.choice([-1.0, 1.0])
    x[o[0], :, 8:] = 0
    x[o[0], :, 12:, :, 0] = rng.choice([-1.0, 1.0], (8, 4, C)) * 2.0 ** -30
    x[o[0], :, 12, :, 2] = 2.0 ** -30
    u = d["u"].reshape(N, 8, 16, 8, 16, 4)
    u[:, :, :, :, :4] = 0
    w = np.zeros((N, 8, 16, 4, 8, 16, 4), np.float32)
    for g in range(8):
        for j in range(4):
            u[:, g, 2 * j, g, j, 0] = (1.125 * k).astype(np.float32).astype(BF)
            u[:, g, 2 * j + 1, g, j, 0] = k.astype(BF)
            w[:, g, 12 + j, 0, g, 8 + j, 0] = 1.125 * 2.0 ** -8
            w[:, g, 12 + j, 1, g, 8 + (j + 1) % 4, 0] = -1.25 * 2.0 ** -8
        w[:, g, 12, 1, g, 12, 2] = 2.0 ** 5
    u[o[0], :, :, :, :4] = 0
    for g in range(8):
        for j in range(4):
            u[o[0], g, 8 + j, g, j, 0] = 1.125 * 2.0 ** -30
            u[o[0], g, 8 + (j + 1) % 4, g, j, 1] = 2.0 ** -30
    return {"x": x.reshape(N, 128, 4 * C).astype(BF), "u": u.reshape(N, 128, 512), "v": d["v"], **lists(rng), **weights(rng, w.astype(BF))}
def setup_inputs_odd(rng):
    d = numbers_of(rng)
    x = np.zeros((N, 8, 16, C, 4), np.float32)
    x[:, :, 0, :, 1] = 1.96875 * 2.0 ** 8 * rng.choice([-1.0, 1.0], (N, 8, C))
    x[:, :, :4, :, 0] = -(8 + rng.integers(0, 2, (N, 8, 4, C))) * 2.0 ** -8
    x[:, :, 4:8, :, 0] = 8 * 2.0 ** -8
    a = np.exp2(rng.integers(-3, 4, 8).astype(np.float32))[None, :, None]
    x[:, :, 8, :, 0] = -2.953125 * a
    x[:, :, 12, :, 0] = -1.125 * a
    x[:, :, 14, :, 0] = -0.0703125 * a
    u = d["u"].reshape(N, 8, 16, 8, 16, 4)
    u[:, :, :, :, :4] = 0
    w = np.zeros((N, 8, 16, 4, 8, 16, 4), np.float32)
    for g in range(8):
        for j in range(4):
            u[:, g, j, g, j, 0] = 1.0
            u[:, g, 4 + j, g, j, 0] = 1.0
            w[:, g, 14, j, g, 9, 0] = -2.0 ** (j - 5)
        w[:, g, 12, 0, g, 8, 0] = -28.0
    return {"x": x.reshape(N, 128, 4 * C).astype(BF), "u": u.reshape(N, 128, 512), "v": d["v"], **lists(rng), **weights(rng, w.astype(BF))}
def setup_inputs_ends(rng):
    d = numbers_of(rng)
    o, e = rng.permutation(N) % 4, rng.permutation(N) % 4
    s = rng.choice([-1.0, 1.0], (N, 128, C, 4))
    s[o == 0] = -1
    s[o == 1] = rng.choice([-1.0, 1.0], (N, 1, C, 1))[o == 1]
    for r in range(N):
        if o[r] == 3: s[r, ::8, :, 0] = 1
    x = s * (0.955 + 0.02 * rng.random((N, 128, C, 4))) * 2.0 ** 30
    x[o == 3] = s[o == 3] * 2.0 ** -30
    size = np.where(o == 3, 2.0 ** -30, 2.0 ** 30)
    a = np.stack([rng.permutation(32).reshape(8, 4) % 2 * 2.0 - 1.0 for r in range(N)]) * size[:, None, None]
    u = d["u"].reshape(N, 128, 8, 16, 4)
    u[:, :, :, :4] = a.astype(np.float32).astype(BF)[:, None, :, :, None]
    v = rng.choice([-1.0, 1.0], (N, 128, 512)) * size[:, None, None]
    c = np.arange(C)
    plain, pairs = [c, c[::-1], (c + 1) % C], [c[::-1], c ^ 1, (c + HALF) % C]
    k = orders(rng)
    for r in range(N):
        if e[r] < 3:
            for n in range(3): k[n][r] = plain[(e[r] + n) % 3]
            k[3][r] = pairs[e[r]]
    h = np.where(o == 3, 32.0, -0.125)[:, None] * np.ones((1, 128))
    for r in range(N):
        if o[r] == 3:
            h[r, 14::16] = 2.0 ** -8
            h[r, 15::16] = 2.0 ** 8
        else: h[r, 15::16] = 0
    w = np.zeros((N, 128, 4, 128, 4), np.float32)
    i = np.arange(128)
    for b in range(4): w[:, i, b, i, b] = h
    return {"x": x.astype(np.float32).reshape(N, 128, 4 * C).astype(BF), "u": u.reshape(N, 128, 512), "v": v.astype(np.float32).astype(BF), **stored(k), **weights(rng, w.astype(BF))}
def setup_inputs_spread(rng):
    d = setup_inputs(rng)
    d["x"] = wide(rng, N, 128, 4 * C, cols=6)
    return d
def check_inputs(d):
    b = []
    for k in ("x", "u", "v"):
        a = np.abs(d[k].astype(np.float32))
        if not (np.isfinite(a).all() and ((a == 0) | (a >= 2.0 ** -30) & (a <= 2.0 ** 30)).all()): b.append("a value of " + k)
    for k in ("lg", "pb", "fd"):
        if not (np.sort(d[k].reshape(N, 8, C), axis=2) == np.arange(C)).all(): b.append(k + ": no permutation")
    for r in range(N):
        e = gentries(d["ex"][r])
        if not ((e >= 0) & (e < C)).all(): b.append("an entry of ex")
        elif (e == np.arange(C)).any() or (at(e, e) != np.arange(C)).any(): b.append("ex: no pairs")
    none, least, most = [emit(mx_ref.quantize(np.full((128, 16), k, np.float32).astype(BF)))[1][0, 0] for k in (0.0, 2.0 ** -8, 2.0 ** 8)]
    for r in range(N):
        if ((d["wc"][r] == 0x7F) | (d["wc"][r] == 0xFF)).any(): b.append("wc: a code that is no number")
        s = mx_ref.live(d["ws"][r])
        if ((s != none) & ((s < least) | (s > most))).any(): b.append("ws: a scale out of range")
        if (((d["wc"][r].reshape(16, 8, 512, 4) & 0x7F) != 0) & (s == none)[:, None, :, None]).any(): b.append("wc: a code other than zero under the scale of zeros")
    return b
def at(t, e):
    return np.take_along_axis(t, e.astype(np.int64), axis=1)
def reference(x, u, v, lg, pb, fd, ex, wc, ws):
    qu = [mx_ref.quantize(u[r]) for r in range(N)]
    lay = [pk(wc[r], ws[r]) for r in range(N)]
    leg, back, fore, pair = [[gentries(t[r]) for r in range(N)] for t in (lg, pb, fd, ex)]
    now = [x[r] for r in range(N)]
    for mask in MASK:
        made, swapped = [], []
        for r in range(N):
            s = mx_ref.matmul(qu[r], mx_ref.quantize(now[r])).reshape(8, 16, C)
            low = np.minimum(np.arange(C), pair[r])
            turn = [np.where(at(s[:, j], low) < 0, pair[r], np.arange(C)) for j in range(4)]
            for j, b in enumerate((back[r ^ mask], back[r], back[r ^ mask])):
                leg[r] = at(b, at(turn[j], at(leg[r], fore[r])))
            swapped.append(at(back[r], turn[3]))
            z = (gcols(now[r], leg[r]).astype(np.float32) + gcols(now[r], at(leg[r], fore[r])).astype(np.float32)) * np.float32(0.5)
            q = mx_ref.quantize(z.astype(BF))
            made.append(tile([mx_ref.matmul(pick(lay[r], np.arange(128 * b, 128 * b + 128)), q) * np.float32(0.03125) for b in range(4)]))
        new = []
        for r in range(N):
            m = at(fore[r], leg[r])
            far = gcols(decode(mx_ref.quantize(made[r ^ mask])).astype(BF), m[:, :HALF])
            near = gcols(made[r], m[:, HALF:])
            new.append((now[r].astype(np.float32) + np.concatenate([far, near], axis=1).astype(np.float32)).astype(BF))
        now, back = new, swapped
    y, pl = np.zeros((N, 128, C), np.float32), np.zeros((N, 8, 2 * C), np.float32)
    oc, osc = np.zeros((N, 128, 4 * C), np.uint8), np.zeros((N, 16, C), np.uint8)
    for r in range(N):
        q = mx_ref.quantize(now[r])
        y[r] = mx_ref.matmul(mx_ref.quantize(v[r]), q)
        pl[r] = np.concatenate([leg[r], back[r]], axis=1)
        oc[r], osc[r] = emit(q)
    return {"y": y, "pl": pl, "oc": oc, "osc": osc}

@@ -1,0 +1,468 @@
+from concourse.mybir import dt, AluOpType as Op, ActivationFunctionType as Act
+
+C, HALF = 288, 144
+MASK = [4, 1, 2]
+K = 65536.0
+_F = {}
+_n = 0
+for _name, _w in (("TM", 288), ("A1", 288), ("A2", 288), ("A0", 576), ("IOT", 288), ("ER", 288), ("FR", 288), ("FF", 288),
+                  ("F3", 288), ("F3S", 288), ("KW", 24), ("CW", 24), ("C1B", 24), ("EXF", 24), ("LOWF", 24), ("D1", 24),
+                  ("D1P", 24), ("PMF", 8), ("PM1", 8), ("T15", 8), ("INV", 8), ("INV4", 8)):
+    _F[_name] = _n
+    _n += _w
+_L = {"pb": 0, "ex": 24, "fd": 48, "lg": 72, "PI": 96, "PM": 104, "UL": 112}
+_U = {"FU": 0, "F3U": 32, "EXU": 64, "LGU": 96, "LOW": 128, "FH": 160, "ULU": 192}
+
+SCRATCH = {
+    "CF": ("sbuf", [128, _n], "float32"), "LI": ("sbuf", [128, 144], "int32"), "CU": ("sbuf", [128, 224], "uint16"),
+    "ut": ("sbuf", [128, 512], "bfloat16"), "vt": ("sbuf", [128, 512], "bfloat16"),
+    "uq": ("sbuf", [128, 128], "float8_e4m3fn_x4"), "us": ("sbuf", [128, 128], "uint8"),
+    "uq2": ("sbuf", [128, 512], "float8_e4m3fn_x4"), "us2": ("sbuf", [128, 512], "uint8"),
+    "vq": ("sbuf", [128, 128], "float8_e4m3fn_x4"), "vs": ("sbuf", [128, 128], "uint8"),
+    "wq": ("sbuf", [128, 512], "float8_e4m3fn_x4"), "wp": ("sbuf", [128, 512], "uint8"),
+    "ONE": ("sbuf", [128, 128], "bfloat16"), "IDM": ("sbuf", [128, 128], "bfloat16"), "ET": ("sbuf", [128, 2048], "bfloat16"),
+    "EQ": ("sbuf", [128, 512], "float8_e4m3fn_x4"), "ES": ("sbuf", [128, 512], "uint8"),
+    "A0B": ("sbuf", [128, 288], "bfloat16"),
+    "M": ("sbuf", [128, 1152], "bfloat16"), "RB": ("sbuf", [128, 1152], "bfloat16"), "SB": ("sbuf", [128, 1152], "bfloat16"),
+    "SR": ("sbuf", [128, 576], "float32"), "ERO": ("sbuf", [128, 576], "float32"), "SE": ("sbuf", [128, 576], "float32"),
+    "SY": ("sbuf", [128, 288], "float32"), "WB": ("sbuf", [128, 864], "float32"), "PP": ("sbuf", [128, 288], "float32"),
+    "KR": ("sbuf", [128, 288], "float32"), "KC": ("sbuf", [128, 288], "float32"),
+    "EA": ("sbuf", [128, 40], "float32"), "DM": ("sbuf", [128, 40], "float32"), "LF": ("sbuf", [128, 40], "float32"),
+    "QS": ("sbuf", [128, 192], "float32"), "TU": ("sbuf", [128, 128], "uint16"),
+    "Y4": ("sbuf", [128, 128], "uint16"), "YW": ("sbuf", [128, 32], "uint16"),
+    "PLB": ("sbuf", [128, 576], "float32"), "YO": ("sbuf", [128, 288], "float32"),
+    "PS": ("psum", [128, 4096], "float32"),
+}
+for _r in range(4):
+    SCRATCH["X%d" % _r] = ("sbuf", [128, 1152], "bfloat16")
+    SCRATCH["XQ%d" % _r] = ("sbuf", [128, 288], "float8_e4m3fn_x4")
+    SCRATCH["XS%d" % _r] = ("sbuf", [128, 288], "uint8")
+for _r in range(3):
+    for _name, _w, _d in (("V", 1152, "bfloat16"), ("VC", 1152, "bfloat16"), ("Z", 1152, "bfloat16"), ("H", 1152, "bfloat16"), ("HP", 576, "bfloat16"),
+                          ("ZQ", 288, "float8_e4m3fn_x4"), ("ZS", 288, "uint8"), ("HQ", 144, "float8_e4m3fn_x4"),
+                          ("HS", 144, "uint8"), ("HL", 144, "float8_e4m3fn_x4"), ("HM", 144, "uint8"),
+                          ("KS", 16, "uint16"), ("KL", 16, "uint16"), ("KO", 16, "uint16"), ("LP", 32, "uint16"),
+                          ("AB", 40, "float32"), ("AU", 64, "uint16"), ("DP", 40, "float32"), ("LU", 64, "uint16"),
+                          ("ROW", 576, "float32"), ("YR", 288, "float32")):
+        SCRATCH["%s%d" % (_name, _r)] = ("sbuf", [128, _w], _d)
+
+SEMAPHORES = ["cV", "cS", "cT", "cG", "out", "rl"] + ["ld%d" % i for i in range(12)] + \
+    ["a%s%d" % (k, r) for k in ("k", "p", "c", "s") for r in range(3)]
+
+
+def rank_program(g, core, T, topo):
+    rank = T.rank_of(core)
+    if rank is None:
+        return
+    eng = {"V": g.vector, "S": g.scalar, "T": g.tensor, "G": g, "Y": g.sync}
+    csem = {"V": "cV", "S": "cS", "T": "cT", "G": "cG"}
+    count = {"cV": 0, "cS": 0, "cT": 0, "cG": 0, "out": 0, "rl": 0}
+    know = {q: {} for q in eng}
+    uses = {}
+    order = [0]
+
+    def A(name, lo, hi, ph=None):
+        ap = T[name][:, lo:hi] if ph is None else T[name][:, lo + ph:hi:4]
+        return ap, [(name, lo, hi, ph)]
+
+    def CF(name, w=18, lo=0):
+        return A("CF", _F[name] + lo, _F[name] + lo + w)
+
+    def LI(name, w=18):
+        return A("LI", _L[name], _L[name] + w)
+
+    def CU(name, w=18, lo=0):
+        return A("CU", _U[name] + lo, _U[name] + lo + w)
+
+    def E16(name, lo, hi):
+        return T[name][:, lo + 15:hi:16], [(name, lo, hi, None)]
+
+    def B8(name, lo, hi):
+        return T[name][:, lo:hi].bitcast(dt.uint8), [(name, lo, hi, None)]
+
+    def ind(win, off):
+        return win[0].indirect(off[0]), win[1] + off[1]
+
+    def BANK(i, n):
+        return T["PS"][:, 512 * i:512 * i + n], [("PS", i, i + 1, None)]
+
+    def deps(q, ins, outs):
+        found = {}
+        for regs, w in ((ins, False), (outs, True)):
+            for (name, lo, hi, ph) in regs:
+                for (l2, h2, p2, w2, op) in uses.get(name, ()):
+                    if hi <= l2 or h2 <= lo or not (ph is None or p2 is None or ph == p2):
+                        continue
+                    same = op["q"] == q and op["compute"]
+                    if name == "PS":
+                        if same:
+                            continue
+                    elif not (w or w2) or (same and w and not w2):
+                        continue
+                    found[op["n"]] = op
+        for n in sorted(found, reverse=True):
+            op = found[n]
+            if know[q].get(op["sem"], 0) < op["val"]:
+                eng[q].wait_ge(T.sem[op["sem"]], op["val"])
+                know[q][op["sem"]] = op["val"]
+                for s, v in op["know"].items():
+                    if know[q].get(s, 0) < v:
+                        know[q][s] = v
+
+    def note(op, ins, outs):
+        order[0] += 1
+        op["n"] = order[0]
+        for regs, w in ((ins, False), (outs, True)):
+            for (name, lo, hi, ph) in regs:
+                uses.setdefault(name, []).append((lo, hi, ph, w, op))
+
+    def regs_of(args):
+        out = []
+        for a in args:
+            out += a[1]
+        return out
+
+    def emit(q, fn, outs, ins):
+        ri, ro = regs_of(ins), regs_of(outs)
+        deps(q, ri, ro)
+        s = csem[q]
+        count[s] += 1
+        fn(eng[q]).then_inc(T.sem[s], 1)
+        note({"q": q, "compute": True, "sem": s, "val": count[s], "know": dict(know[q])}, ri, ro)
+
+    def load(q, sem, dst, src):
+        deps(q, [], dst[1])
+        eng[q].dma_start(dst[0], src).then_inc(T.sem[sem], 16)
+        note({"q": q, "compute": False, "sem": sem, "val": 16, "know": dict(know[q])}, [], dst[1])
+
+    def store(q, dst, src):
+        deps(q, src[1], [])
+        eng[q].dma_start(dst, src[0]).then_inc(T.sem.out, 16)
+        count["out"] += 16
+
+    def send(to, dst, src, sem):
+        c = T.cores[to]
+        deps("G", src[1], [])
+        rid, pid = topo.addr(c, core)
+        n = len(topo.engines(core, c))
+        g.remote_dma(dst[0], src[0], T.sem[sem], T.sem.rl, pid, rid, topo.mask(core, c))
+        count["rl"] += n
+        note({"q": "G", "compute": False, "sem": sem, "val": n, "know": {}}, [], dst[1])
+
+    def sc(a):
+        return a[0] if isinstance(a, tuple) else a
+
+    def more(*a):
+        return [b for b in a if isinstance(b, tuple)]
+
+    def ts(out, in0, s1, s2, op0, op1=None):
+        if op1 is None:
+            emit("V", lambda e: e.tensor_scalar(out[0], in0[0], sc(s1), None, op0), [out], [in0] + more(s1))
+        else:
+            emit("V", lambda e: e.tensor_scalar(out[0], in0[0], sc(s1), sc(s2), op0, op1), [out], [in0] + more(s1, s2))
+
+    def tt(out, a, b, op):
+        emit("V", lambda e: e.tensor_tensor(out[0], a[0], b[0], op), [out], [a, b])
+
+    def cp(out, a):
+        emit("V", lambda e: e.tensor_copy(out[0], a[0]), [out], [a])
+
+    def act(out, a, f, scale=1.0):
+        emit("S", lambda e: e.activation(out[0], a[0], f, scale=scale), [out], [a])
+
+    def scan(out, data, n, bits=False):
+        d0 = A("A0B", 0, n) if bits else CF("A0", n)
+        emit("V", lambda e: e.tensor_tensor_scan(out[0], d0[0], data[0], 0.0, Op.mult, Op.add), [out], [d0, data])
+
+    def quant(qn, sn, lo, hi, src):
+        a, b = A(qn, lo, hi), A(sn, lo, hi)
+        emit("V", lambda e: e.quantize_mx(a[0], b[0], src[0]), [a, b], [src])
+
+    def mm(bank, wn, sn, wlo, xn, pn, lo, hi):
+        o = BANK(bank, hi - lo)
+        ins = [A(wn, wlo, wlo + 128), A(sn, wlo, wlo + 128), A(xn, lo, hi), A(pn, lo, hi)]
+        emit("T", lambda e: e.matmul_mx(o[0], ins[0][0], ins[1][0], ins[2][0], ins[3][0], True, True), [o], ins)
+
+    def iota(out, pattern, base, mult, f32):
+        if f32:
+            emit("G", lambda e: e.iota(out[0], pattern, base, mult, allow_small_or_imprecise_dtypes=True), [out], [])
+        else:
+            emit("G", lambda e: e.iota(out[0], pattern, base, mult), [out], [])
+
+    def value(out, sc_name, lo, hi):
+        ts(out, E16(sc_name, lo, hi), CF("INV", 1), 0.25, Op.mult, Op.add)
+
+    load("Y", "ld0", LI("pb"), T.pb[:, :])
+    load("S", "ld1", A("ut", 0, 512), T.u[:, :])
+    load("Y", "ld2", LI("ex"), T.ex[:, :])
+    load("S", "ld3", LI("fd"), T.fd[:, :])
+    load("Y", "ld4", A("X0", 0, 1152), T.x[:, :])
+    load("S", "ld5", LI("lg"), T.lg[:, :])
+    load("Y", "ld6", B8("wq", 0, 512), T.wc[:, :])
+    load("Y", "ld7", A("wp", 0, 512), T.ws[:, :])
+    load("Y", "ld8", A("vt", 0, 512), T.v[:, :])
+
+    iota(LI("PI", 1), [[0, 1]], 0, 1, False)
+    iota(CF("TM", 288), [[0, 18], [1, 16]], 0, 0, True)
+    iota(CF("KW"), [[16, 18]], 0, 0, True)
+    iota(LI("UL", 32), [[1, 4], [16, 8]], 0, 0, False)
+    iota(CF("IOT", 288), [[1, 288]], 0, 0, True)
+
+    emit("V", lambda e: e.memset(T.ONE[:, :], 1.0), [A("ONE", 0, 128)], [])
+    ts(LI("PM", 1), LI("PI", 1), 15, None, Op.bitwise_and)
+    cp(CF("PMF", 1), LI("PM", 1))
+    ts(CF("PM1", 1), CF("PMF", 1), 1.0, None, Op.add)
+    ts(CF("T15", 1), CF("PMF", 1), 15.0, 1.0 - 1.0 / K, Op.is_equal, Op.mult)
+    ts(CF("INV", 1), CF("T15", 1), 1.0 / K, None, Op.add)
+    ts(CF("INV4", 1), CF("INV", 1), 4.0, None, Op.mult)
+    ts(CF("A1", 288), CF("TM", 288), CF("PMF", 1), 1.0, Op.subtract, Op.is_ge)
+    ts(CF("A2", 288), CF("TM", 288), CF("PM1", 1), K - 1.0, Op.is_equal, Op.mult)
+    tt(CF("A0", 288), CF("A1", 288), CF("A2", 288), Op.add)
+    cp(A("A0B", 0, 288), CF("A0", 288))
+    act(CF("A0", 288, 288), CF("A0", 288), Act.Copy)
+
+    cp(A("AU0", 0, 18), LI("pb"))
+    send(rank ^ MASK[0], A("LP0", 0, 18), A("AU0", 0, 18), "ap0")
+    emit("G", lambda e: e.affine_select(T.IDM[:, :], T.ONE[:, :], [[-1, 128]], Op.is_equal, 0.0, 0, 1),
+         [A("IDM", 0, 128)], [A("ONE", 0, 128)])
+
+    cp(CU("ULU", 32), LI("UL", 32))
+    cp(CU("FU"), LI("fd"))
+    cp(CU("EXU"), LI("ex"))
+    act(CF("FR", 288), ind(CF("IOT", 288), CU("FU")), Act.Copy)
+    act(CF("FF", 288), ind(CF("FR", 288), CU("FU")), Act.Copy)
+    act(CF("F3", 288), ind(CF("FF", 288), CU("FU")), Act.Copy)
+    cp(CF("ER", 288), ind(CF("IOT", 288), CU("EXU")))
+    quant("uq", "us", 0, 128, A("ut", 0, 512))
+    emit("V", lambda e: e.tensor_copy(T.uq2[:, 0:512].bitcast(dt.uint32),
+                                      T.uq[:, 0:128].bitcast(dt.uint32).indirect(CU("ULU", 32)[0])),
+         [A("uq2", 0, 512)], [A("uq", 0, 128), CU("ULU", 32)])
+    emit("S", lambda e: e.activation(T.us2[:, 0:512], T.us[:, 0:128].indirect(CU("ULU", 32)[0]), Act.Copy),
+         [A("us2", 0, 512)], [A("us", 0, 128), CU("ULU", 32)])
+    quant("XQ0", "XS0", 0, 288, A("X0", 0, 1152))
+    for j in (2, 1, 0, 3):
+        mm(j, "uq2", "us2", 128 * j, "XQ0", "XS0", 0, 288)
+
+    def eprep(r, lo, hi):
+        scan(A("SE", 16 * lo, 16 * hi), A("ERO", 16 * lo, 16 * hi), 16 * (hi - lo))
+        value(A("EA", lo, hi), "SE", 16 * lo, 16 * hi)
+        tt(A("LF", lo, hi), A("EA", lo, hi), A("AB%d" % r, lo, hi), Op.min)
+        cp(A("LU%d" % r, lo, hi), A("LF", lo, hi))
+        tt(A("DM", lo, hi), A("EA", lo, hi), A("AB%d" % r, lo, hi), Op.subtract)
+        ts(A("DP%d" % r, lo, hi), A("DM", lo, hi), CF("INV", 1), None, Op.mult)
+
+    cp(A("ERO", 0, 288), ind(CF("ER", 288), A("AU0", 0, 18)))
+    ts(A("AB0", 0, 18), LI("pb"), 1.0, 0.25, Op.mult, Op.add)
+    eprep(0, 0, 18)
+    cp(CU("LGU"), LI("lg"))
+    cp(A("YR0", 0, 288), ind(CF("IOT", 288), CU("LGU")))
+    scan(CF("F3S", 288), CF("F3", 288), 288)
+    ts(CU("F3U"), (T.CF[:, _F["F3S"] + 15:_F["F3S"] + 288:16], CF("F3S", 288)[1]), CF("INV", 1), 0.25, Op.mult, Op.add)
+    act(A("ROW0", 288, 576), ind(A("YR0", 0, 288), CU("F3U")), Act.Copy)
+    ts(CF("CW"), CF("KW"), CF("PMF", 1), None, Op.add)
+    ts(CF("C1B"), CF("CW"), 0.25, None, Op.add)
+    cp(CF("EXF"), LI("ex"))
+    tt(CF("LOWF"), CF("EXF"), CF("CW"), Op.min)
+    cp(CU("LOW"), CF("LOWF"))
+    tt(CF("D1"), CF("EXF"), CF("CW"), Op.subtract)
+    ts(CF("D1P"), CF("D1"), CF("INV", 1), None, Op.mult)
+    scan(A("SR", 288, 576), A("ROW0", 288, 576), 288)
+    value(A("AB0", 18, 36), "SR", 288, 576)
+    cp(A("AU0", 18, 36), A("AB0", 18, 36))
+    act(A("ERO", 288, 576), ind(CF("ER", 288), A("AU0", 18, 36)), Act.Copy)
+    act(A("ROW0", 0, 288), ind(CF("IOT", 288), A("AU0", 0, 18)), Act.Copy)
+
+    def msig(q, j, lo, hi):
+        o, i = A("M", 288 * j + lo, 288 * j + hi), BANK(j, hi - lo)
+        if q == "V":
+            ts(o, i, 0.0, None, Op.is_lt)
+        else:
+            act(o, i, Act.Sign, -1.0)
+
+    def rbit(q, j, lst):
+        o, i = A("RB", 288 * j, 288 * j + 288), ind(A("M", 288 * j, 288 * j + 288), lst)
+        if q == "V":
+            ts(o, i, 0.0, None, Op.max)
+        else:
+            act(o, i, Act.Relu)
+
+    def sbit(j):
+        scan(A("SB", 288 * j, 288 * j + 288), A("RB", 288 * j, 288 * j + 288), 288, bits=True)
+
+    def choose(j, dp, ab):
+        a, b = A("QS", 48 * j, 48 * j + 18), A("QS", 48 * j + 24, 48 * j + 42)
+        tt(a, E16("SB", 288 * j, 288 * j + 288), dp, Op.mult)
+        tt(b, a, ab, Op.add)
+        cp(A("TU", 32 * j, 32 * j + 18), b)
+
+    def tu(j):
+        return A("TU", 32 * j, 32 * j + 18)
+
+    def prow(r):
+        act(A("PP", 0, 288), ind(CF("IOT", 288), A("LP%d" % r, 0, 18)), Act.Copy)
+
+    for r in range(3):
+        other = rank ^ MASK[r]
+        x, xn, last = "X%d" % r, "X%d" % (r + 1), r == 2
+        v, vc, z, h, hp = "V%d" % r, "VC%d" % r, "Z%d" % r, "H%d" % r, "HP%d" % r
+        ks, kl, ko = "KS%d" % r, "KL%d" % r, "KO%d" % r
+        lu, dp, ab = "LU%d" % r, "DP%d" % r, "AB%d" % r
+        hi = C if r == 0 else HALF
+        msig("V", 2, 0, hi)
+        msig("S", 1, 0, hi)
+        rbit("V", 2, A(lu, 0, 18))
+        rbit("S", 1, CU("LOW"))
+        msig("S", 0, 0, hi)
+        msig("S", 3, 0, hi)
+        sbit(2)
+        choose(2, A(dp, 0, 18), A(ab, 0, 18))
+        if r == 0:
+            eprep(0, 18, 36)
+            prow(0)
+        act(A("WB", 0, 288), ind(A("PP", 0, 288), tu(2)), Act.Copy)
+        sbit(1)
+        choose(1, CF("D1P"), CF("C1B"))
+        act(A("WB", 288, 576), ind(A("WB", 0, 288), tu(1)), Act.Copy)
+        act(A("WB", 576, 864), ind(A("WB", 288, 576), A("LP%d" % r, 0, 18)), Act.Copy)
+        rbit("V", 0, A(lu, 18, 36))
+        sbit(0)
+        choose(0, A(dp, 18, 36), A(ab, 18, 36))
+        yrow = A("PLB", 0, 288) if last else A("YR%d" % (r + 1), 0, 288)
+        act(yrow, ind(A("WB", 576, 864), tu(0)), Act.Copy)
+        rbit("V", 3, CU("LOW"))
+        scan(A("SY", 0, 288), yrow, 288)
+        value(A("YW", 0, 9), "SY", 0, 144)
+
+        def y4(t):
+            ts(A("Y4", 18 * t, 18 * t + 18), E16("SY", 0, 288), CF("INV4", 1), t + 0.1, Op.mult, Op.add)
+
+        def gv(t):
+            act(A(v, 288 * t, 288 * t + 288), ind(A(x, 0, 1152), A("Y4", 18 * t, 18 * t + 18)), Act.Copy, 0.5)
+
+        def gz(t, a, b):
+            f = CU("FU") if (a, b) == (0, C) else CU("FH", 9, 10 * (a // HALF))
+            w = A(v, 288 * t, 288 * t + 288)
+            tt(A(z, 4 * a, 4 * b, t), ind(w, f), A(vc, 288 * t + a, 288 * t + b), Op.add)
+
+        def gc(q, t):
+            o, i = A(vc, 288 * t, 288 * t + 288), A(v, 288 * t, 288 * t + 288)
+            if q == "V":
+                cp(o, i)
+            else:
+                act(o, i, Act.Copy)
+
+        y4(0)
+        act(A("KR", 0, 144), ind(CF("FR", 288), A("YW", 0, 9)), Act.Copy)
+        gv(0)
+        for t in (1, 2, 3):
+            y4(t)
+        scan(A("KC", 0, 144), A("KR", 0, 144), 144)
+        value(A(ks, 0, 9), "KC", 0, 144)
+        send(other, A(kl, 0, 9), A(ks, 0, 9), "ak%d" % r)
+        sbit(3)
+        choose(3, CF("D1P"), CF("C1B"))
+        value(A("YW", 10, 19), "SY", 144, 288)
+        if r == 0:
+            cp(CU("FH", 9, 0), A("LI", _L["fd"], _L["fd"] + 9))
+            cp(CU("FH", 9, 10), A("LI", _L["fd"] + 9, _L["fd"] + 18))
+        gv(1)
+        for t in (2, 3):
+            gv(t)
+            gc("S", t)
+        nrow = A("PLB", 288, 576) if last else A("ROW%d" % (r + 1), 0, 288)
+        act(nrow, ind(A("ROW%d" % r, 0, 288), tu(3)), Act.Copy)
+        if last:
+            store("Y", T.pl[:, :], (T.PLB[0:128:16, :], [("PLB", 0, 576, None)]))
+        zq, zs = "ZQ%d" % r, "ZS%d" % r
+        for t in (0, 1, 2):
+            if t < 2:
+                gc("V", t)
+            gz(t, 0, C)
+        gz(3, 0, HALF)
+        quant(zq, zs, 0, HALF, A(z, 0, 576))
+        gz(3, HALF, C)
+        quant(zq, zs, HALF, C, A(z, 576, 1152))
+
+        def ev(q, hf, b):
+            o, i = A(h, 288 * b + 144 * hf, 288 * b + 144 * hf + 144), BANK(4 * hf + b, HALF)
+            if q == "V":
+                ts(o, i, 0.03125, None, Op.mult)
+            else:
+                act(o, i, Act.Copy, 0.03125)
+
+        for b in range(4):
+            mm(b, "wq", "wp", 128 * b, zq, zs, 0, HALF)
+            ev("S", 0, b)
+        for b in range(4):
+            mm(4 + b, "wq", "wp", 128 * b, zq, zs, HALF, C)
+            ev("S" if b == 3 else "V", 1, b)
+        for b in (0, 2, 1, 3):
+            i = ind(A(h, 288 * b, 288 * b + 288), A(kl, 0, 9))
+            if b < 2:
+                cp(A(hp, 0, 576, b), i)
+            else:
+                act(A(hp, 0, 576, b), i, Act.Copy)
+        hq, hs, hl, hm = "HQ%d" % r, "HS%d" % r, "HL%d" % r, "HM%d" % r
+        quant(hq, hs, 0, HALF, A(hp, 0, 576))
+        send(other, B8(hl, 0, HALF), B8(hq, 0, HALF), "ac%d" % r)
+        send(other, A(hm, 0, HALF), A(hs, 0, HALF), "as%d" % r)
+        if not last:
+            nr = r + 1
+            rown, abn, aun = "ROW%d" % nr, "AB%d" % nr, "AU%d" % nr
+            scan(A("SR", 0, 288), A(rown, 0, 288), 288)
+            value(A(abn, 0, 18), "SR", 0, 288)
+            cp(A(aun, 0, 18), A(abn, 0, 18))
+            send(rank ^ MASK[nr], A("LP%d" % nr, 0, 18), A(aun, 0, 18), "ap%d" % nr)
+        act(A("KR", 144, 288), ind(CF("FR", 288), A("YW", 10, 19)), Act.Copy)
+        if not last:
+            act(A(rown, 288, 576), ind(yrow, CU("F3U")), Act.Copy)
+            scan(A("SR", 288, 576), A(rown, 288, 576), 288)
+            value(A(abn, 18, 36), "SR", 288, 576)
+            cp(A(aun, 18, 36), A(abn, 18, 36))
+            act(A("ERO", 0, 576), ind(CF("ER", 288), A(aun, 0, 36)), Act.Copy)
+        scan(A("KC", 144, 288), A("KR", 144, 288), 144)
+        value(A(ko, 0, 9), "KC", 144, 288)
+        for b in range(4):
+            tt(A(xn, 576, 1152, b), ind(A(h, 288 * b, 288 * b + 288), A(ko, 0, 9)), A(x, 576, 1152, b), Op.add)
+        xq, xs = "XQ%d" % (r + 1), "XS%d" % (r + 1)
+        quant(xq, xs, HALF, C, A(xn, 576, 1152))
+
+        def yout(a, b, bank):
+            mm(bank, "vq", "vs", 0, xq, xs, a, b)
+            act(A("YO", a, b), BANK(bank, b - a), Act.Copy)
+
+        def stores(a, b):
+            store("Y", T.oc[:, 4 * a:4 * b], B8(xq, a, b))
+            for k in range(4):
+                store("Y", T.osc[4 * k:4 * k + 4, a:b], (T[xs][32 * k:32 * k + 4, a:b], [(xs, a, b, None)]))
+
+        if last:
+            quant("vq", "vs", 0, 128, A("vt", 0, 512))
+            yout(HALF, C, 0)
+            stores(HALF, C)
+            store("S", T.y[:, HALF:C], A("YO", HALF, C))
+        else:
+            for j in (2, 1, 0, 3):
+                mm(j, "uq2", "us2", 128 * j, xq, xs, HALF, C)
+                msig("S", j, HALF, C)
+            eprep(r + 1, 0, 36)
+        if r == 0:
+            emit("V", lambda e: e.memset(T.ET[:, :], 0.0), [A("ET", 0, 2048)], [])
+            for b in range(4):
+                cp(A("ET", 512 * b, 512 * b + 512, b), A("IDM", 0, 128))
+            quant("EQ", "ES", 0, 512, A("ET", 0, 2048))
+        if not last:
+            prow(r + 1)
+        for b in range(4):
+            mm(4 + b, "EQ", "ES", 128 * b, hl, hm, 0, HALF)
+            tt(A(xn, 0, 576, b), A(x, 0, 576, b), BANK(4 + b, HALF), Op.add)
+        quant(xq, xs, 0, HALF, A(xn, 0, 576))
+        if last:
+            yout(0, HALF, 1)
+            stores(0, HALF)
+            store("S", T.y[:, 0:HALF], A("YO", 0, HALF))
+        else:
+            for j in (2, 1, 0, 3):
+                mm(j, "uq2", "us2", 128 * j, xq, xs, 0, HALF)
+    for s in ("cV", "cS", "cT", "cG", "out", "rl"):
+        g.wait_ge(T.sem[s], count[s])

@@ -3,15 +3,16 @@ from concourse.mybir import dt, AluOpType as Op, ActivationFunctionType as Act
 C, HALF = 288, 144
 MASK = [4, 1, 2]
 K = 65536.0
+SLOT = {2: 0, 1: 1, 0: 2, 3: 3}
 _F = {}
 _n = 0
-for _name, _w in (("TM", 288), ("A1", 288), ("A2", 288), ("A0", 576), ("IOT", 288), ("ER", 288), ("FR", 288), ("FF", 288),
-                  ("F3", 288), ("F3S", 288), ("KW", 24), ("CW", 24), ("C1B", 24), ("EXF", 24), ("LOWF", 24), ("D1", 24),
-                  ("D1P", 24), ("PMF", 8), ("PM1", 8), ("T15", 8), ("INV", 8), ("INV4", 8)):
+for _name, _w in (("TM", 288), ("A1", 288), ("A2", 288), ("A0", 288), ("IOT", 288), ("ER", 288), ("FR", 288), ("FF", 288),
+                  ("F3", 288), ("F3S", 288), ("KW", 24), ("CW", 24), ("EXF", 24), ("LOWF", 24), ("D1", 24),
+                  ("PMF", 8), ("PM1", 8), ("T15", 8), ("INV", 8)):
     _F[_name] = _n
     _n += _w
 _L = {"pb": 0, "ex": 24, "fd": 48, "lg": 72, "PI": 96, "PM": 104, "UL": 112}
-_U = {"FU": 0, "F3U": 32, "EXU": 64, "LGU": 96, "LOW": 128, "FH": 160, "ULU": 192}
+_U = {"FU": 0, "F3U": 32, "EXU": 64, "LGU": 96, "FH": 160, "ULU": 192}
 
 SCRATCH = {
     "CF": ("sbuf", [128, _n], "float32"), "LI": ("sbuf", [128, 144], "int32"), "CU": ("sbuf", [128, 224], "uint16"),
@@ -20,16 +21,18 @@ SCRATCH = {
     "uq2": ("sbuf", [128, 512], "float8_e4m3fn_x4"), "us2": ("sbuf", [128, 512], "uint8"),
     "vq": ("sbuf", [128, 128], "float8_e4m3fn_x4"), "vs": ("sbuf", [128, 128], "uint8"),
     "wq": ("sbuf", [128, 512], "float8_e4m3fn_x4"), "wp": ("sbuf", [128, 512], "uint8"),
-    "ONE": ("sbuf", [128, 128], "bfloat16"), "IDM": ("sbuf", [128, 128], "bfloat16"), "ET": ("sbuf", [128, 2048], "bfloat16"),
+    "ONE": ("sbuf", [128, 512], "bfloat16"), "ET": ("sbuf", [128, 2048], "bfloat16"),
     "EQ": ("sbuf", [128, 512], "float8_e4m3fn_x4"), "ES": ("sbuf", [128, 512], "uint8"),
-    "A0B": ("sbuf", [128, 288], "bfloat16"),
+    "A0B": ("sbuf", [128, 576], "bfloat16"),
     "M": ("sbuf", [128, 1152], "bfloat16"), "RB": ("sbuf", [128, 1152], "bfloat16"), "SB": ("sbuf", [128, 1152], "bfloat16"),
     "SR": ("sbuf", [128, 576], "float32"), "ERO": ("sbuf", [128, 576], "float32"), "SE": ("sbuf", [128, 576], "float32"),
-    "SY": ("sbuf", [128, 288], "float32"), "WB": ("sbuf", [128, 864], "float32"), "PP": ("sbuf", [128, 288], "float32"),
-    "KR": ("sbuf", [128, 288], "float32"), "KC": ("sbuf", [128, 288], "float32"),
-    "EA": ("sbuf", [128, 40], "float32"), "DM": ("sbuf", [128, 40], "float32"), "LF": ("sbuf", [128, 40], "float32"),
-    "QS": ("sbuf", [128, 192], "float32"), "TU": ("sbuf", [128, 128], "uint16"),
-    "Y4": ("sbuf", [128, 128], "uint16"), "YW": ("sbuf", [128, 32], "uint16"),
+    "SY": ("sbuf", [128, 288], "float32"), "PP": ("sbuf", [128, 288], "float32"),
+    "WA": ("sbuf", [128, 288], "float32"), "WB": ("sbuf", [128, 288], "float32"),
+    "KR": ("sbuf", [128, 304], "float32"), "KC": ("sbuf", [128, 288], "float32"),
+    "EA": ("sbuf", [128, 56], "float32"), "DM": ("sbuf", [128, 56], "float32"), "LF": ("sbuf", [128, 56], "float32"),
+    "AB": ("sbuf", [128, 56], "float32"), "DP": ("sbuf", [128, 56], "float32"), "LU": ("sbuf", [128, 64], "uint16"),
+    "QS": ("sbuf", [128, 144], "float32"), "TU": ("sbuf", [128, 96], "uint16"), "YW": ("sbuf", [128, 32], "uint16"),
+    "YG": ("sbuf", [128, 288], "float32"), "YF": ("sbuf", [128, 288], "float32"),
     "PLB": ("sbuf", [128, 576], "float32"), "YO": ("sbuf", [128, 288], "float32"),
     "PS": ("psum", [128, 4096], "float32"),
 }
@@ -38,12 +41,12 @@ for _r in range(4):
     SCRATCH["XQ%d" % _r] = ("sbuf", [128, 288], "float8_e4m3fn_x4")
     SCRATCH["XS%d" % _r] = ("sbuf", [128, 288], "uint8")
 for _r in range(3):
-    for _name, _w, _d in (("V", 1152, "bfloat16"), ("VC", 1152, "bfloat16"), ("Z", 1152, "bfloat16"), ("H", 1152, "bfloat16"), ("HP", 576, "bfloat16"),
+    for _name, _w, _d in (("V", 1152, "bfloat16"), ("VC", 1152, "bfloat16"), ("Z", 1152, "bfloat16"), ("H", 1152, "bfloat16"),
+                          ("HP", 576, "bfloat16"), ("XP", 1152, "bfloat16"),
                           ("ZQ", 288, "float8_e4m3fn_x4"), ("ZS", 288, "uint8"), ("HQ", 144, "float8_e4m3fn_x4"),
                           ("HS", 144, "uint8"), ("HL", 144, "float8_e4m3fn_x4"), ("HM", 144, "uint8"),
                           ("KS", 16, "uint16"), ("KL", 16, "uint16"), ("KO", 16, "uint16"), ("LP", 32, "uint16"),
-                          ("AB", 40, "float32"), ("AU", 64, "uint16"), ("DP", 40, "float32"), ("LU", 64, "uint16"),
-                          ("ROW", 576, "float32"), ("YR", 288, "float32")):
+                          ("AU", 64, "uint16"), ("ROW", 576, "float32"), ("YR", 288, "float32")):
         SCRATCH["%s%d" % (_name, _r)] = ("sbuf", [128, _w], _d)
 
 SEMAPHORES = ["cV", "cS", "cT", "cG", "out", "rl"] + ["ld%d" % i for i in range(12)] + \
@@ -167,8 +170,14 @@ def rank_program(g, core, T, topo):
     def cp(out, a):
         emit("V", lambda e: e.tensor_copy(out[0], a[0]), [out], [a])
 
-    def act(out, a, f, scale=1.0):
+    def act(out, a, f=Act.Copy, scale=1.0):
         emit("S", lambda e: e.activation(out[0], a[0], f, scale=scale), [out], [a])
+
+    def move(q, out, a):
+        if q == "V":
+            cp(out, a)
+        else:
+            act(out, a)
 
     def scan(out, data, n, bits=False):
         d0 = A("A0B", 0, n) if bits else CF("A0", n)
@@ -189,50 +198,64 @@ def rank_program(g, core, T, topo):
         else:
             emit("G", lambda e: e.iota(out[0], pattern, base, mult), [out], [])
 
+    def planar(r, a, b):
+        for t in range(4):
+            o, i = A("XP%d" % r, 288 * t + a, 288 * t + b), A("X%d" % r, 4 * a, 4 * b, t)
+            emit("G", lambda e: e.affine_select(o[0], i[0], [[0, b - a]], Op.is_gt, 0.0, 1, 0), [o], [i])
+
     def value(out, sc_name, lo, hi):
         ts(out, E16(sc_name, lo, hi), CF("INV", 1), 0.25, Op.mult, Op.add)
 
+    def chain(out, lo, win, off, o0, split=True):
+        if split:
+            cp(A(out, lo, lo + 160), ind(win, A(off, o0, o0 + 10)))
+            act(A(out, lo + 160, lo + 288), ind(win, A(off, o0 + 10, o0 + 18)))
+        else:
+            act(A(out, lo, lo + 288), ind(win, A(off, o0, o0 + 18)))
+
     load("Y", "ld0", LI("pb"), T.pb[:, :])
     load("S", "ld1", A("ut", 0, 512), T.u[:, :])
-    load("Y", "ld2", LI("ex"), T.ex[:, :])
-    load("S", "ld3", LI("fd"), T.fd[:, :])
     load("Y", "ld4", A("X0", 0, 1152), T.x[:, :])
     load("S", "ld5", LI("lg"), T.lg[:, :])
+    load("S", "ld3", LI("fd"), T.fd[:, :])
+    load("Y", "ld2", LI("ex"), T.ex[:, :])
     load("Y", "ld6", B8("wq", 0, 512), T.wc[:, :])
     load("Y", "ld7", A("wp", 0, 512), T.ws[:, :])
     load("Y", "ld8", A("vt", 0, 512), T.v[:, :])
 
     iota(LI("PI", 1), [[0, 1]], 0, 1, False)
     iota(CF("TM", 288), [[0, 18], [1, 16]], 0, 0, True)
-    iota(CF("KW"), [[16, 18]], 0, 0, True)
-    iota(LI("UL", 32), [[1, 4], [16, 8]], 0, 0, False)
     iota(CF("IOT", 288), [[1, 288]], 0, 0, True)
+    iota(LI("UL", 32), [[1, 4], [16, 8]], 0, 0, False)
+    iota(CF("KW"), [[16, 18]], 0, 0, True)
 
-    emit("V", lambda e: e.memset(T.ONE[:, :], 1.0), [A("ONE", 0, 128)], [])
+    emit("V", lambda e: e.memset(T.ONE[:, :], 1.0), [A("ONE", 0, 512)], [])
     ts(LI("PM", 1), LI("PI", 1), 15, None, Op.bitwise_and)
     cp(CF("PMF", 1), LI("PM", 1))
     ts(CF("PM1", 1), CF("PMF", 1), 1.0, None, Op.add)
     ts(CF("T15", 1), CF("PMF", 1), 15.0, 1.0 - 1.0 / K, Op.is_equal, Op.mult)
-    ts(CF("INV", 1), CF("T15", 1), 1.0 / K, None, Op.add)
-    ts(CF("INV4", 1), CF("INV", 1), 4.0, None, Op.mult)
     ts(CF("A1", 288), CF("TM", 288), CF("PMF", 1), 1.0, Op.subtract, Op.is_ge)
     ts(CF("A2", 288), CF("TM", 288), CF("PM1", 1), K - 1.0, Op.is_equal, Op.mult)
+    ts(CF("INV", 1), CF("T15", 1), 1.0 / K, None, Op.add)
     tt(CF("A0", 288), CF("A1", 288), CF("A2", 288), Op.add)
-    cp(A("A0B", 0, 288), CF("A0", 288))
-    act(CF("A0", 288, 288), CF("A0", 288), Act.Copy)
+    act(A("A0B", 0, 288), CF("A0", 288))
+    act(A("A0B", 288, 576), CF("A0", 288))
+    cp(CU("ULU", 32), LI("UL", 32))
+    ts(CF("CW"), CF("KW"), CF("PMF", 1), None, Op.add)
+    for i in range(3):
+        ts(A("AB", 18 * i, 18 * i + 18), CF("CW"), 0.25, None, Op.add)
 
     cp(A("AU0", 0, 18), LI("pb"))
     send(rank ^ MASK[0], A("LP0", 0, 18), A("AU0", 0, 18), "ap0")
-    emit("G", lambda e: e.affine_select(T.IDM[:, :], T.ONE[:, :], [[-1, 128]], Op.is_equal, 0.0, 0, 1),
-         [A("IDM", 0, 128)], [A("ONE", 0, 128)])
+    planar(0, 0, C)
 
-    cp(CU("ULU", 32), LI("UL", 32))
-    cp(CU("FU"), LI("fd"))
-    cp(CU("EXU"), LI("ex"))
-    act(CF("FR", 288), ind(CF("IOT", 288), CU("FU")), Act.Copy)
-    act(CF("FF", 288), ind(CF("FR", 288), CU("FU")), Act.Copy)
-    act(CF("F3", 288), ind(CF("FF", 288), CU("FU")), Act.Copy)
-    cp(CF("ER", 288), ind(CF("IOT", 288), CU("EXU")))
+    def onehot(b):
+        emit("G", lambda e: e.affine_select(T.ET[:, 512 * b:512 * b + 512], T.ONE[:, :], [[-1, 512]], Op.is_equal, 0.0, b, 4),
+             [A("ET", 512 * b, 512 * b + 512)], [A("ONE", 0, 512)])
+
+    for b in range(4):
+        onehot(b)
+
     quant("uq", "us", 0, 128, A("ut", 0, 512))
     emit("V", lambda e: e.tensor_copy(T.uq2[:, 0:512].bitcast(dt.uint32),
                                       T.uq[:, 0:128].bitcast(dt.uint32).indirect(CU("ULU", 32)[0])),
@@ -242,35 +265,14 @@ def rank_program(g, core, T, topo):
     quant("XQ0", "XS0", 0, 288, A("X0", 0, 1152))
     for j in (2, 1, 0, 3):
         mm(j, "uq2", "us2", 128 * j, "XQ0", "XS0", 0, 288)
-
-    def eprep(r, lo, hi):
-        scan(A("SE", 16 * lo, 16 * hi), A("ERO", 16 * lo, 16 * hi), 16 * (hi - lo))
-        value(A("EA", lo, hi), "SE", 16 * lo, 16 * hi)
-        tt(A("LF", lo, hi), A("EA", lo, hi), A("AB%d" % r, lo, hi), Op.min)
-        cp(A("LU%d" % r, lo, hi), A("LF", lo, hi))
-        tt(A("DM", lo, hi), A("EA", lo, hi), A("AB%d" % r, lo, hi), Op.subtract)
-        ts(A("DP%d" % r, lo, hi), A("DM", lo, hi), CF("INV", 1), None, Op.mult)
-
-    cp(A("ERO", 0, 288), ind(CF("ER", 288), A("AU0", 0, 18)))
-    ts(A("AB0", 0, 18), LI("pb"), 1.0, 0.25, Op.mult, Op.add)
-    eprep(0, 0, 18)
     cp(CU("LGU"), LI("lg"))
-    cp(A("YR0", 0, 288), ind(CF("IOT", 288), CU("LGU")))
-    scan(CF("F3S", 288), CF("F3", 288), 288)
-    ts(CU("F3U"), (T.CF[:, _F["F3S"] + 15:_F["F3S"] + 288:16], CF("F3S", 288)[1]), CF("INV", 1), 0.25, Op.mult, Op.add)
-    act(A("ROW0", 288, 576), ind(A("YR0", 0, 288), CU("F3U")), Act.Copy)
-    ts(CF("CW"), CF("KW"), CF("PMF", 1), None, Op.add)
-    ts(CF("C1B"), CF("CW"), 0.25, None, Op.add)
+    cp(CU("FU"), LI("fd"))
     cp(CF("EXF"), LI("ex"))
     tt(CF("LOWF"), CF("EXF"), CF("CW"), Op.min)
-    cp(CU("LOW"), CF("LOWF"))
+    cp(A("LU", 18, 36), CF("LOWF"))
     tt(CF("D1"), CF("EXF"), CF("CW"), Op.subtract)
-    ts(CF("D1P"), CF("D1"), CF("INV", 1), None, Op.mult)
-    scan(A("SR", 288, 576), A("ROW0", 288, 576), 288)
-    value(A("AB0", 18, 36), "SR", 288, 576)
-    cp(A("AU0", 18, 36), A("AB0", 18, 36))
-    act(A("ERO", 288, 576), ind(CF("ER", 288), A("AU0", 18, 36)), Act.Copy)
-    act(A("ROW0", 0, 288), ind(CF("IOT", 288), A("AU0", 0, 18)), Act.Copy)
+    for i in range(3):
+        ts(A("DP", 18 * i, 18 * i + 18), CF("D1"), CF("INV", 1), None, Op.mult)
 
     def msig(q, j, lo, hi):
         o, i = A("M", 288 * j + lo, 288 * j + hi), BANK(j, hi - lo)
@@ -280,64 +282,72 @@ def rank_program(g, core, T, topo):
             act(o, i, Act.Sign, -1.0)
 
     def rbit(q, j, lst):
-        o, i = A("RB", 288 * j, 288 * j + 288), ind(A("M", 288 * j, 288 * j + 288), lst)
+        s = SLOT[j]
+        o, i = A("RB", 288 * s, 288 * s + 288), ind(A("M", 288 * j, 288 * j + 288), lst)
         if q == "V":
             ts(o, i, 0.0, None, Op.max)
         else:
             act(o, i, Act.Relu)
 
-    def sbit(j):
-        scan(A("SB", 288 * j, 288 * j + 288), A("RB", 288 * j, 288 * j + 288), 288, bits=True)
+    def choose(s, n, at):
+        scan(A("SB", 288 * s, 288 * (s + n)), A("RB", 288 * s, 288 * (s + n)), 288 * n, bits=True)
+        a, b = A("QS", 18 * s, 18 * (s + n)), A("QS", 72 + 18 * s, 72 + 18 * (s + n))
+        tt(a, E16("SB", 288 * s, 288 * (s + n)), A("DP", at, at + 18 * n), Op.mult)
+        tt(b, a, A("AB", at, at + 18 * n), Op.add)
+        cp(A("TU", 18 * s, 18 * (s + n)), b)
 
-    def choose(j, dp, ab):
-        a, b = A("QS", 48 * j, 48 * j + 18), A("QS", 48 * j + 24, 48 * j + 42)
-        tt(a, E16("SB", 288 * j, 288 * j + 288), dp, Op.mult)
-        tt(b, a, ab, Op.add)
-        cp(A("TU", 32 * j, 32 * j + 18), b)
-
-    def tu(j):
-        return A("TU", 32 * j, 32 * j + 18)
-
-    def prow(r):
-        act(A("PP", 0, 288), ind(CF("IOT", 288), A("LP%d" % r, 0, 18)), Act.Copy)
+    LOW = A("LU", 18, 36)
 
     for r in range(3):
         other = rank ^ MASK[r]
         x, xn, last = "X%d" % r, "X%d" % (r + 1), r == 2
         v, vc, z, h, hp = "V%d" % r, "VC%d" % r, "Z%d" % r, "H%d" % r, "HP%d" % r
-        ks, kl, ko = "KS%d" % r, "KL%d" % r, "KO%d" % r
-        lu, dp, ab = "LU%d" % r, "DP%d" % r, "AB%d" % r
-        hi = C if r == 0 else HALF
-        msig("V", 2, 0, hi)
-        msig("S", 1, 0, hi)
-        rbit("V", 2, A(lu, 0, 18))
-        rbit("S", 1, CU("LOW"))
-        msig("S", 0, 0, hi)
-        msig("S", 3, 0, hi)
-        sbit(2)
-        choose(2, A(dp, 0, 18), A(ab, 0, 18))
+        ks, kl, ko, au, lp = "KS%d" % r, "KL%d" % r, "KO%d" % r, "AU%d" % r, "LP%d" % r
+        yn = "PLB" if last else "YR%d" % (r + 1)
+        yrow = A(yn, 0, 288)
+        pp = A("PP", 0, 288)
         if r == 0:
-            eprep(0, 18, 36)
-            prow(0)
-        act(A("WB", 0, 288), ind(A("PP", 0, 288), tu(2)), Act.Copy)
-        sbit(1)
-        choose(1, CF("D1P"), CF("C1B"))
-        act(A("WB", 288, 576), ind(A("WB", 0, 288), tu(1)), Act.Copy)
-        act(A("WB", 576, 864), ind(A("WB", 288, 576), A("LP%d" % r, 0, 18)), Act.Copy)
-        rbit("V", 0, A(lu, 18, 36))
-        sbit(0)
-        choose(0, A(dp, 18, 36), A(ab, 18, 36))
-        yrow = A("PLB", 0, 288) if last else A("YR%d" % (r + 1), 0, 288)
-        act(yrow, ind(A("WB", 576, 864), tu(0)), Act.Copy)
-        rbit("V", 3, CU("LOW"))
+            msig("V", 2, 0, C)
+            msig("S", 1, 0, C)
+            rbit("V", 2, LOW)
+            rbit("S", 1, LOW)
+            msig("S", 0, 0, C)
+            choose(0, 2, 0)
+            rbit("S", 0, LOW)
+            chain("YR0", 0, CF("IOT", 288), "CU", _U["LGU"])
+            chain("YG", 0, A("YR0", 0, 288), "CU", _U["FU"])
+            choose(2, 1, 36)
+            chain("YF", 0, A("YG", 0, 288), "CU", _U["FU"])
+            chain("ROW0", 288, A("YF", 0, 288), "CU", _U["FU"])
+            scan(A("SR", 288, 576), A("ROW0", 288, 576), 288)
+            value(A("AU0", 18, 36), "SR", 288, 576)
+            act(CF("FR", 288), ind(CF("IOT", 288), CU("FU")))
+            quant("EQ", "ES", 0, 512, A("ET", 0, 2048))
+            chain("PP", 0, CF("IOT", 288), lp, 0)
+            chain("WA", 0, pp, "TU", 0)
+            chain("WB", 0, A("WA", 0, 288), "AU0", 0)
+            chain("WA", 0, A("WB", 0, 288), "TU", 18)
+            chain("WB", 0, A("WA", 0, 288), lp, 0)
+            chain("WA", 0, A("WB", 0, 288), "TU", 36)
+            chain(yn, 0, A("WA", 0, 288), "AU0", 18)
+        else:
+            msig("V", 2, 0, HALF)
+            msig("S", 1, 0, HALF)
+            rbit("V", 2, A("LU", 0, 18))
+            rbit("S", 1, LOW)
+            msig("S", 0, 0, HALF)
+            choose(0, 2, 0)
+            rbit("S", 0, A("LU", 36, 54))
+            chain("WA", 0, pp, "TU", 0)
+            choose(2, 1, 36)
+            chain("WB", 0, A("WA", 0, 288), "TU", 18, False)
+            chain("WA", 0, A("WB", 0, 288), lp, 0)
+            chain(yn, 0, A("WA", 0, 288), "TU", 36)
         scan(A("SY", 0, 288), yrow, 288)
-        value(A("YW", 0, 9), "SY", 0, 144)
-
-        def y4(t):
-            ts(A("Y4", 18 * t, 18 * t + 18), E16("SY", 0, 288), CF("INV4", 1), t + 0.1, Op.mult, Op.add)
+        value(A("YW", 0, 18), "SY", 0, 288)
 
         def gv(t):
-            act(A(v, 288 * t, 288 * t + 288), ind(A(x, 0, 1152), A("Y4", 18 * t, 18 * t + 18)), Act.Copy, 0.5)
+            act(A(v, 288 * t, 288 * t + 288), ind(A("XP%d" % r, 288 * t, 288 * t + 288), A("YW", 0, 18)), Act.Copy, 0.5)
 
         def gz(t, a, b):
             f = CU("FU") if (a, b) == (0, C) else CU("FH", 9, 10 * (a // HALF))
@@ -345,23 +355,13 @@ def rank_program(g, core, T, topo):
             tt(A(z, 4 * a, 4 * b, t), ind(w, f), A(vc, 288 * t + a, 288 * t + b), Op.add)
 
         def gc(q, t):
-            o, i = A(vc, 288 * t, 288 * t + 288), A(v, 288 * t, 288 * t + 288)
-            if q == "V":
-                cp(o, i)
-            else:
-                act(o, i, Act.Copy)
+            move(q, A(vc, 288 * t, 288 * t + 288), A(v, 288 * t, 288 * t + 288))
 
-        y4(0)
-        act(A("KR", 0, 144), ind(CF("FR", 288), A("YW", 0, 9)), Act.Copy)
+        act(A("KR", 0, 144), ind(CF("FR", 288), A("YW", 0, 9)))
         gv(0)
-        for t in (1, 2, 3):
-            y4(t)
         scan(A("KC", 0, 144), A("KR", 0, 144), 144)
         value(A(ks, 0, 9), "KC", 0, 144)
         send(other, A(kl, 0, 9), A(ks, 0, 9), "ak%d" % r)
-        sbit(3)
-        choose(3, CF("D1P"), CF("C1B"))
-        value(A("YW", 10, 19), "SY", 144, 288)
         if r == 0:
             cp(CU("FH", 9, 0), A("LI", _L["fd"], _L["fd"] + 9))
             cp(CU("FH", 9, 10), A("LI", _L["fd"] + 9, _L["fd"] + 18))
@@ -369,10 +369,9 @@ def rank_program(g, core, T, topo):
         for t in (2, 3):
             gv(t)
             gc("S", t)
-        nrow = A("PLB", 288, 576) if last else A("ROW%d" % (r + 1), 0, 288)
-        act(nrow, ind(A("ROW%d" % r, 0, 288), tu(3)), Act.Copy)
-        if last:
-            store("Y", T.pl[:, :], (T.PLB[0:128:16, :], [("PLB", 0, 576, None)]))
+        msig("S", 3, 0, C if r == 0 else HALF)
+        rbit("S", 3, LOW)
+        act(A("KR", 144, 304), ind(CF("FR", 288), A("YW", 8, 18)))
         zq, zs = "ZQ%d" % r, "ZS%d" % r
         for t in (0, 1, 2):
             if t < 2:
@@ -395,73 +394,96 @@ def rank_program(g, core, T, topo):
             ev("S", 0, b)
         for b in range(4):
             mm(4 + b, "wq", "wp", 128 * b, zq, zs, HALF, C)
-            ev("S" if b == 3 else "V", 1, b)
-        for b in (0, 2, 1, 3):
-            i = ind(A(h, 288 * b, 288 * b + 288), A(kl, 0, 9))
-            if b < 2:
-                cp(A(hp, 0, 576, b), i)
-            else:
-                act(A(hp, 0, 576, b), i, Act.Copy)
+            ev("S" if b < 2 else "V", 1, b)
+        for b in range(4):
+            move("S" if b < 2 else "V", A(hp, 0, 576, b), ind(A(h, 288 * b, 288 * b + 288), A(kl, 0, 9)))
         hq, hs, hl, hm = "HQ%d" % r, "HS%d" % r, "HL%d" % r, "HM%d" % r
         quant(hq, hs, 0, HALF, A(hp, 0, 576))
         send(other, B8(hl, 0, HALF), B8(hq, 0, HALF), "ac%d" % r)
         send(other, A(hm, 0, HALF), A(hs, 0, HALF), "as%d" % r)
-        if not last:
-            nr = r + 1
-            rown, abn, aun = "ROW%d" % nr, "AB%d" % nr, "AU%d" % nr
-            scan(A("SR", 0, 288), A(rown, 0, 288), 288)
-            value(A(abn, 0, 18), "SR", 0, 288)
-            cp(A(aun, 0, 18), A(abn, 0, 18))
-            send(rank ^ MASK[nr], A("LP%d" % nr, 0, 18), A(aun, 0, 18), "ap%d" % nr)
-        act(A("KR", 144, 288), ind(CF("FR", 288), A("YW", 10, 19)), Act.Copy)
-        if not last:
-            act(A(rown, 288, 576), ind(yrow, CU("F3U")), Act.Copy)
-            scan(A("SR", 288, 576), A(rown, 288, 576), 288)
-            value(A(abn, 18, 36), "SR", 288, 576)
-            cp(A(aun, 18, 36), A(abn, 18, 36))
-            act(A("ERO", 0, 576), ind(CF("ER", 288), A(aun, 0, 36)), Act.Copy)
-        scan(A("KC", 144, 288), A("KR", 144, 288), 144)
-        value(A(ko, 0, 9), "KC", 144, 288)
-        for b in range(4):
+        def own(b):
             tt(A(xn, 576, 1152, b), ind(A(h, 288 * b, 288 * b + 288), A(ko, 0, 9)), A(x, 576, 1152, b), Op.add)
-        xq, xs = "XQ%d" % (r + 1), "XS%d" % (r + 1)
-        quant(xq, xs, HALF, C, A(xn, 576, 1152))
 
-        def yout(a, b, bank):
-            mm(bank, "vq", "vs", 0, xq, xs, a, b)
-            act(A("YO", a, b), BANK(bank, b - a), Act.Copy)
-
-        def stores(a, b):
-            store("Y", T.oc[:, 4 * a:4 * b], B8(xq, a, b))
-            for k in range(4):
-                store("Y", T.osc[4 * k:4 * k + 4, a:b], (T[xs][32 * k:32 * k + 4, a:b], [(xs, a, b, None)]))
-
+        nr = r + 1
+        xq, xs = "XQ%d" % nr, "XS%d" % nr
+        rown, aun = ("PLB" if last else "ROW%d" % nr), "AU%d" % nr
+        plo = 288 if last else 0
+        prow_old = A("ROW%d" % r, 0, 288)
+        if r == 0:
+            act(prow_old, ind(CF("IOT", 288), A("AU0", 0, 18)))
+        choose(3, 1, 18)
+        act(A(rown, plo, plo + 288), ind(prow_old, A("TU", 54, 72)))
+        scan(A("KC", 144, 288), A("KR", 160, 304), 144)
+        value(A(ko, 0, 9), "KC", 144, 288)
+        own(0)
         if last:
+            store("Y", T.pl[:, :], (T.PLB[0:128:16, :], [("PLB", 0, 576, None)]))
+            for b in (1, 2, 3):
+                own(b)
+            quant(xq, xs, HALF, C, A(xn, 576, 1152))
             quant("vq", "vs", 0, 128, A("vt", 0, 512))
-            yout(HALF, C, 0)
-            stores(HALF, C)
-            store("S", T.y[:, HALF:C], A("YO", HALF, C))
         else:
+            scan(A("SR", 0, 288), A(rown, 0, 288), 288)
+            value(A("AB", 0, 18), "SR", 0, 288)
+            cp(A(aun, 0, 18), A("AB", 0, 18))
+            send(rank ^ MASK[nr], A("LP%d" % nr, 0, 18), A(aun, 0, 18), "ap%d" % nr)
+            if r == 0:
+                cp(CU("EXU"), LI("ex"))
+                act(CF("FF", 288), ind(CF("FR", 288), CU("FU")))
+                act(CF("F3", 288), ind(CF("FF", 288), CU("FU")))
+                act(CF("ER", 288), ind(CF("IOT", 288), CU("EXU")))
+                own(1)
+                scan(CF("F3S", 288), CF("F3", 288), 288)
+                ts(CU("F3U"), (T.CF[:, _F["F3S"] + 15:_F["F3S"] + 288:16], CF("F3S", 288)[1]), CF("INV", 1), 0.25, Op.mult, Op.add)
+                ts(A("EA", 18, 36), CF("EXF"), 0.25, None, Op.add)
+            act(A(rown, 288, 576), ind(yrow, CU("F3U")))
+            act(A("ERO", 0, 288), ind(CF("ER", 288), A(aun, 0, 18)))
+            if r > 0:
+                own(1)
+            scan(A("SR", 288, 576), A(rown, 288, 576), 288)
+            value(A("AB", 36, 54), "SR", 288, 576)
+            cp(A(aun, 18, 36), A("AB", 36, 54))
+            act(A("ERO", 288, 576), ind(CF("ER", 288), A(aun, 18, 36)))
+            own(2)
+            own(3)
+            quant(xq, xs, HALF, C, A(xn, 576, 1152))
+            planar(nr, HALF, C)
+            for i, at in ((0, 0), (1, 36)):
+                scan(A("SE", 288 * i, 288 * i + 288), A("ERO", 288 * i, 288 * i + 288), 288)
+                value(A("EA", at, at + 18), "SE", 288 * i, 288 * i + 288)
+            tt(A("LF", 0, 54), A("EA", 0, 54), A("AB", 0, 54), Op.min)
+            tt(A("DM", 0, 54), A("EA", 0, 54), A("AB", 0, 54), Op.subtract)
+            cp(A("LU", 0, 54), A("LF", 0, 54))
+            ts(A("DP", 0, 54), A("DM", 0, 54), CF("INV", 1), None, Op.mult)
             for j in (2, 1, 0, 3):
                 mm(j, "uq2", "us2", 128 * j, xq, xs, HALF, C)
                 msig("S", j, HALF, C)
-            eprep(r + 1, 0, 36)
-        if r == 0:
-            emit("V", lambda e: e.memset(T.ET[:, :], 0.0), [A("ET", 0, 2048)], [])
-            for b in range(4):
-                cp(A("ET", 512 * b, 512 * b + 512, b), A("IDM", 0, 128))
-            quant("EQ", "ES", 0, 512, A("ET", 0, 2048))
-        if not last:
-            prow(r + 1)
+            chain("PP", 0, CF("IOT", 288), "LP%d" % nr, 0, False)
+
+        def yout(a, b, bank):
+            mm(bank, "vq", "vs", 0, xq, xs, a, b)
+            act(A("YO", a, b), BANK(bank, b - a))
+
+        def osc(q, k, a, b):
+            store(q, T.osc[4 * k:4 * k + 4, a:b], (T[xs][32 * k:32 * k + 4, a:b], [(xs, a, b, None)]))
+
+        def stores(a, b):
+            yout(a, b, a // HALF)
+            store("Y", T.oc[:, 4 * a:4 * b], B8(xq, a, b))
+            store("S", T.y[:, a:b], A("YO", a, b))
+            for k in range(4):
+                osc("Y" if k < 3 else "S", k, a, b)
+
+        if last:
+            stores(HALF, C)
         for b in range(4):
             mm(4 + b, "EQ", "ES", 128 * b, hl, hm, 0, HALF)
             tt(A(xn, 0, 576, b), A(x, 0, 576, b), BANK(4 + b, HALF), Op.add)
         quant(xq, xs, 0, HALF, A(xn, 0, 576))
         if last:
-            yout(0, HALF, 1)
             stores(0, HALF)
-            store("S", T.y[:, 0:HALF], A("YO", 0, HALF))
         else:
+            planar(nr, 0, HALF)
             for j in (2, 1, 0, 3):
                 mm(j, "uq2", "us2", 128 * j, xq, xs, 0, HALF)
     for s in ("cV", "cS", "cT", "cG", "out", "rl"):

@@ -256,6 +256,9 @@ def rank_program(g, core, T, topo):
     for b in range(4):
         onehot(b)
 
+    cp(CU("LGU"), LI("lg"))
+    cp(CU("FU"), LI("fd"))
+    chain("YR0", 0, CF("IOT", 288), "CU", _U["LGU"], False)
     quant("uq", "us", 0, 128, A("ut", 0, 512))
     emit("V", lambda e: e.tensor_copy(T.uq2[:, 0:512].bitcast(dt.uint32),
                                       T.uq[:, 0:128].bitcast(dt.uint32).indirect(CU("ULU", 32)[0])),
@@ -265,8 +268,7 @@ def rank_program(g, core, T, topo):
     quant("XQ0", "XS0", 0, 288, A("X0", 0, 1152))
     for j in (2, 1, 0, 3):
         mm(j, "uq2", "us2", 128 * j, "XQ0", "XS0", 0, 288)
-    cp(CU("LGU"), LI("lg"))
-    cp(CU("FU"), LI("fd"))
+    chain("YG", 0, A("YR0", 0, 288), "CU", _U["FU"], False)
     cp(CF("EXF"), LI("ex"))
     tt(CF("LOWF"), CF("EXF"), CF("CW"), Op.min)
     cp(A("LU", 18, 36), CF("LOWF"))
@@ -289,12 +291,16 @@ def rank_program(g, core, T, topo):
         else:
             act(o, i, Act.Relu)
 
-    def choose(s, n, at):
-        scan(A("SB", 288 * s, 288 * (s + n)), A("RB", 288 * s, 288 * (s + n)), 288 * n, bits=True)
+    def choose(s, n, at, between=()):
         a, b = A("QS", 18 * s, 18 * (s + n)), A("QS", 72 + 18 * s, 72 + 18 * (s + n))
-        tt(a, E16("SB", 288 * s, 288 * (s + n)), A("DP", at, at + 18 * n), Op.mult)
-        tt(b, a, A("AB", at, at + 18 * n), Op.add)
-        cp(A("TU", 18 * s, 18 * (s + n)), b)
+        steps = [lambda: scan(A("SB", 288 * s, 288 * (s + n)), A("RB", 288 * s, 288 * (s + n)), 288 * n, bits=True),
+                 lambda: tt(a, E16("SB", 288 * s, 288 * (s + n)), A("DP", at, at + 18 * n), Op.mult),
+                 lambda: tt(b, a, A("AB", at, at + 18 * n), Op.add),
+                 lambda: cp(A("TU", 18 * s, 18 * (s + n)), b)]
+        for i, step in enumerate(steps):
+            step()
+            if i < len(between):
+                between[i]()
 
     LOW = A("LU", 18, 36)
 
@@ -314,15 +320,12 @@ def rank_program(g, core, T, topo):
             msig("S", 0, 0, C)
             choose(0, 2, 0)
             rbit("S", 0, LOW)
-            chain("YR0", 0, CF("IOT", 288), "CU", _U["LGU"])
-            chain("YG", 0, A("YR0", 0, 288), "CU", _U["FU"])
-            choose(2, 1, 36)
             chain("YF", 0, A("YG", 0, 288), "CU", _U["FU"])
+            choose(2, 1, 36)
             chain("ROW0", 288, A("YF", 0, 288), "CU", _U["FU"])
+            act(CF("FR", 288), ind(CF("IOT", 288), CU("FU")))
             scan(A("SR", 288, 576), A("ROW0", 288, 576), 288)
             value(A("AU0", 18, 36), "SR", 288, 576)
-            act(CF("FR", 288), ind(CF("IOT", 288), CU("FU")))
-            quant("EQ", "ES", 0, 512, A("ET", 0, 2048))
             chain("PP", 0, CF("IOT", 288), lp, 0)
             chain("WA", 0, pp, "TU", 0)
             chain("WB", 0, A("WA", 0, 288), "AU0", 0)
@@ -336,6 +339,7 @@ def rank_program(g, core, T, topo):
             rbit("V", 2, A("LU", 0, 18))
             rbit("S", 1, LOW)
             msig("S", 0, 0, HALF)
+            chain("PP", 0, CF("IOT", 288), lp, 0, False)
             choose(0, 2, 0)
             rbit("S", 0, A("LU", 36, 54))
             chain("WA", 0, pp, "TU", 0)
@@ -358,15 +362,15 @@ def rank_program(g, core, T, topo):
             move(q, A(vc, 288 * t, 288 * t + 288), A(v, 288 * t, 288 * t + 288))
 
         act(A("KR", 0, 144), ind(CF("FR", 288), A("YW", 0, 9)))
-        gv(0)
+        ts(A(v, 0, 288), ind(A("XP%d" % r, 0, 288), A("YW", 0, 18)), 0.5, None, Op.mult)
         scan(A("KC", 0, 144), A("KR", 0, 144), 144)
+        gc("V", 0)
         value(A(ks, 0, 9), "KC", 0, 144)
         send(other, A(kl, 0, 9), A(ks, 0, 9), "ak%d" % r)
         if r == 0:
             cp(CU("FH", 9, 0), A("LI", _L["fd"], _L["fd"] + 9))
             cp(CU("FH", 9, 10), A("LI", _L["fd"] + 9, _L["fd"] + 18))
-        gv(1)
-        for t in (2, 3):
+        for t in (1, 2, 3):
             gv(t)
             gc("S", t)
         msig("S", 3, 0, C if r == 0 else HALF)
@@ -374,8 +378,6 @@ def rank_program(g, core, T, topo):
         act(A("KR", 144, 304), ind(CF("FR", 288), A("YW", 8, 18)))
         zq, zs = "ZQ%d" % r, "ZS%d" % r
         for t in (0, 1, 2):
-            if t < 2:
-                gc("V", t)
             gz(t, 0, C)
         gz(3, 0, HALF)
         quant(zq, zs, 0, HALF, A(z, 0, 576))
@@ -395,8 +397,8 @@ def rank_program(g, core, T, topo):
         for b in range(4):
             mm(4 + b, "wq", "wp", 128 * b, zq, zs, HALF, C)
             ev("S" if b < 2 else "V", 1, b)
-        for b in range(4):
-            move("S" if b < 2 else "V", A(hp, 0, 576, b), ind(A(h, 288 * b, 288 * b + 288), A(kl, 0, 9)))
+        for q, b, at, to in (("S", 0, 0, 9), ("V", 2, 0, 9), ("S", 1, 0, 9), ("V", 3, 0, 4), ("S", 3, 4, 9)):
+            move(q, A(hp, 64 * at, 64 * to, b), ind(A(h, 288 * b, 288 * b + 288), A(kl, at, to)))
         hq, hs, hl, hm = "HQ%d" % r, "HS%d" % r, "HL%d" % r, "HM%d" % r
         quant(hq, hs, 0, HALF, A(hp, 0, 576))
         send(other, B8(hl, 0, HALF), B8(hq, 0, HALF), "ac%d" % r)
@@ -411,11 +413,11 @@ def rank_program(g, core, T, topo):
         prow_old = A("ROW%d" % r, 0, 288)
         if r == 0:
             act(prow_old, ind(CF("IOT", 288), A("AU0", 0, 18)))
-        choose(3, 1, 18)
+        if not last:
+            chain("YG", 0, yrow, "CU", _U["FU"], False)
+        choose(3, 1, 18, (lambda: scan(A("KC", 144, 288), A("KR", 160, 304), 144),
+                          lambda: value(A(ko, 0, 9), "KC", 144, 288), lambda: own(0)))
         act(A(rown, plo, plo + 288), ind(prow_old, A("TU", 54, 72)))
-        scan(A("KC", 144, 288), A("KR", 160, 304), 144)
-        value(A(ko, 0, 9), "KC", 144, 288)
-        own(0)
         if last:
             store("Y", T.pl[:, :], (T.PLB[0:128:16, :], [("PLB", 0, 576, None)]))
             for b in (1, 2, 3):
@@ -423,42 +425,35 @@ def rank_program(g, core, T, topo):
             quant(xq, xs, HALF, C, A(xn, 576, 1152))
             quant("vq", "vs", 0, 128, A("vt", 0, 512))
         else:
-            scan(A("SR", 0, 288), A(rown, 0, 288), 288)
-            value(A("AB", 0, 18), "SR", 0, 288)
-            cp(A(aun, 0, 18), A("AB", 0, 18))
-            send(rank ^ MASK[nr], A("LP%d" % nr, 0, 18), A(aun, 0, 18), "ap%d" % nr)
+            own(1)
             if r == 0:
                 cp(CU("EXU"), LI("ex"))
-                act(CF("FF", 288), ind(CF("FR", 288), CU("FU")))
-                act(CF("F3", 288), ind(CF("FF", 288), CU("FU")))
-                act(CF("ER", 288), ind(CF("IOT", 288), CU("EXU")))
-                own(1)
-                scan(CF("F3S", 288), CF("F3", 288), 288)
-                ts(CU("F3U"), (T.CF[:, _F["F3S"] + 15:_F["F3S"] + 288:16], CF("F3S", 288)[1]), CF("INV", 1), 0.25, Op.mult, Op.add)
                 ts(A("EA", 18, 36), CF("EXF"), 0.25, None, Op.add)
-            act(A(rown, 288, 576), ind(yrow, CU("F3U")))
-            act(A("ERO", 0, 288), ind(CF("ER", 288), A(aun, 0, 18)))
-            if r > 0:
-                own(1)
+            scan(A("SR", 0, 288), A(rown, 0, 288), 288)
+            own(2)
+            value(A("AB", 0, 18), "SR", 0, 288)
+            own(3)
+            cp(A(aun, 0, 18), A("AB", 0, 18))
+            send(rank ^ MASK[nr], A("LP%d" % nr, 0, 18), A(aun, 0, 18), "ap%d" % nr)
+            quant(xq, xs, HALF, C, A(xn, 576, 1152))
+            planar(nr, HALF, C)
+            chain("YF", 0, A("YG", 0, 288), "CU", _U["FU"], False)
+            chain(rown, 288, A("YF", 0, 288), "CU", _U["FU"], False)
             scan(A("SR", 288, 576), A(rown, 288, 576), 288)
+            if r == 0:
+                act(CF("ER", 288), ind(CF("IOT", 288), CU("EXU")))
+            act(A("ERO", 0, 288), ind(CF("ER", 288), A(aun, 0, 18)))
             value(A("AB", 36, 54), "SR", 288, 576)
             cp(A(aun, 18, 36), A("AB", 36, 54))
             act(A("ERO", 288, 576), ind(CF("ER", 288), A(aun, 18, 36)))
-            own(2)
-            own(3)
-            quant(xq, xs, HALF, C, A(xn, 576, 1152))
-            planar(nr, HALF, C)
-            for i, at in ((0, 0), (1, 36)):
-                scan(A("SE", 288 * i, 288 * i + 288), A("ERO", 288 * i, 288 * i + 288), 288)
-                value(A("EA", at, at + 18), "SE", 288 * i, 288 * i + 288)
-            tt(A("LF", 0, 54), A("EA", 0, 54), A("AB", 0, 54), Op.min)
-            tt(A("DM", 0, 54), A("EA", 0, 54), A("AB", 0, 54), Op.subtract)
-            cp(A("LU", 0, 54), A("LF", 0, 54))
-            ts(A("DP", 0, 54), A("DM", 0, 54), CF("INV", 1), None, Op.mult)
             for j in (2, 1, 0, 3):
                 mm(j, "uq2", "us2", 128 * j, xq, xs, HALF, C)
                 msig("S", j, HALF, C)
-            chain("PP", 0, CF("IOT", 288), "LP%d" % nr, 0, False)
+            for i, at in ((0, 0), (1, 36)):
+                if r == 0:
+                    quant("EQ", "ES", 256 * i, 256 * i + 256, A("ET", 1024 * i, 1024 * i + 1024))
+                scan(A("SE", 288 * i, 288 * i + 288), A("ERO", 288 * i, 288 * i + 288), 288)
+                value(A("EA", at, at + 18), "SE", 288 * i, 288 * i + 288)
 
         def yout(a, b, bank):
             mm(bank, "vq", "vs", 0, xq, xs, a, b)
@@ -484,6 +479,10 @@ def rank_program(g, core, T, topo):
             stores(0, HALF)
         else:
             planar(nr, 0, HALF)
+            tt(A("LF", 0, 54), A("EA", 0, 54), A("AB", 0, 54), Op.min)
+            tt(A("DM", 0, 54), A("EA", 0, 54), A("AB", 0, 54), Op.subtract)
+            cp(A("LU", 0, 54), A("LF", 0, 54))
+            ts(A("DP", 0, 54), A("DM", 0, 54), CF("INV", 1), None, Op.mult)
             for j in (2, 1, 0, 3):
                 mm(j, "uq2", "us2", 128 * j, xq, xs, 0, HALF)
     for s in ("cV", "cS", "cT", "cG", "out", "rl"):

@@ -207,7 +207,9 @@ def rank_program(g, core, T, topo):
         ts(out, E16(sc_name, lo, hi), CF("INV", 1), 0.25, Op.mult, Op.add)
 
     def chain(out, lo, win, off, o0, split=True):
-        if split:
+        if split == "V":
+            cp(A(out, lo, lo + 288), ind(win, A(off, o0, o0 + 18)))
+        elif split:
             cp(A(out, lo, lo + 160), ind(win, A(off, o0, o0 + 10)))
             act(A(out, lo + 160, lo + 288), ind(win, A(off, o0 + 10, o0 + 18)))
         else:
@@ -238,6 +240,8 @@ def rank_program(g, core, T, topo):
     ts(CF("A2", 288), CF("TM", 288), CF("PM1", 1), K - 1.0, Op.is_equal, Op.mult)
     ts(CF("INV", 1), CF("T15", 1), 1.0 / K, None, Op.add)
     tt(CF("A0", 288), CF("A1", 288), CF("A2", 288), Op.add)
+    cp(A("AU0", 0, 18), LI("pb"))
+    send(rank ^ MASK[0], A("LP0", 0, 18), A("AU0", 0, 18), "ap0")
     act(A("A0B", 0, 288), CF("A0", 288))
     act(A("A0B", 288, 576), CF("A0", 288))
     cp(CU("ULU", 32), LI("UL", 32))
@@ -245,8 +249,6 @@ def rank_program(g, core, T, topo):
     for i in range(3):
         ts(A("AB", 18 * i, 18 * i + 18), CF("CW"), 0.25, None, Op.add)
 
-    cp(A("AU0", 0, 18), LI("pb"))
-    send(rank ^ MASK[0], A("LP0", 0, 18), A("AU0", 0, 18), "ap0")
     planar(0, 0, C)
 
     def onehot(b):
@@ -259,20 +261,26 @@ def rank_program(g, core, T, topo):
     cp(CU("LGU"), LI("lg"))
     cp(CU("FU"), LI("fd"))
     chain("YR0", 0, CF("IOT", 288), "CU", _U["LGU"], False)
+    def stand(j, n):
+        off, o = CU("ULU", 8 * n, 8 * j), (128 * j, 128 * (j + n))
+        emit("V", lambda e: e.tensor_copy(T.uq2[:, o[0]:o[1]].bitcast(dt.uint32),
+                                          T.uq[:, 0:128].bitcast(dt.uint32).indirect(off[0])),
+             [A("uq2", o[0], o[1])], [A("uq", 0, 128), off])
+        emit("S", lambda e: e.activation(T.us2[:, o[0]:o[1]], T.us[:, 0:128].indirect(off[0]), Act.Copy),
+             [A("us2", o[0], o[1])], [A("us", 0, 128), off])
+
+    cp(CF("EXF"), LI("ex"))
     quant("uq", "us", 0, 128, A("ut", 0, 512))
-    emit("V", lambda e: e.tensor_copy(T.uq2[:, 0:512].bitcast(dt.uint32),
-                                      T.uq[:, 0:128].bitcast(dt.uint32).indirect(CU("ULU", 32)[0])),
-         [A("uq2", 0, 512)], [A("uq", 0, 128), CU("ULU", 32)])
-    emit("S", lambda e: e.activation(T.us2[:, 0:512], T.us[:, 0:128].indirect(CU("ULU", 32)[0]), Act.Copy),
-         [A("us2", 0, 512)], [A("us", 0, 128), CU("ULU", 32)])
+    tt(CF("LOWF"), CF("EXF"), CF("CW"), Op.min)
+    tt(CF("D1"), CF("EXF"), CF("CW"), Op.subtract)
+    stand(1, 2)
+    cp(A("LU", 18, 36), CF("LOWF"))
     quant("XQ0", "XS0", 0, 288, A("X0", 0, 1152))
+    chain("YG", 0, A("YR0", 0, 288), "CU", _U["FU"], False)
+    stand(0, 1)
+    stand(3, 1)
     for j in (2, 1, 0, 3):
         mm(j, "uq2", "us2", 128 * j, "XQ0", "XS0", 0, 288)
-    chain("YG", 0, A("YR0", 0, 288), "CU", _U["FU"], False)
-    cp(CF("EXF"), LI("ex"))
-    tt(CF("LOWF"), CF("EXF"), CF("CW"), Op.min)
-    cp(A("LU", 18, 36), CF("LOWF"))
-    tt(CF("D1"), CF("EXF"), CF("CW"), Op.subtract)
     for i in range(3):
         ts(A("DP", 18 * i, 18 * i + 18), CF("D1"), CF("INV", 1), None, Op.mult)
 
@@ -315,24 +323,25 @@ def rank_program(g, core, T, topo):
         if r == 0:
             msig("V", 2, 0, C)
             msig("S", 1, 0, C)
+            chain("YF", 0, A("YG", 0, 288), "CU", _U["FU"], "V")
             rbit("V", 2, LOW)
             rbit("S", 1, LOW)
             msig("S", 0, 0, C)
-            choose(0, 2, 0)
             rbit("S", 0, LOW)
-            chain("YF", 0, A("YG", 0, 288), "CU", _U["FU"])
-            choose(2, 1, 36)
-            chain("ROW0", 288, A("YF", 0, 288), "CU", _U["FU"])
             act(CF("FR", 288), ind(CF("IOT", 288), CU("FU")))
-            scan(A("SR", 288, 576), A("ROW0", 288, 576), 288)
-            value(A("AU0", 18, 36), "SR", 288, 576)
-            chain("PP", 0, CF("IOT", 288), lp, 0)
-            chain("WA", 0, pp, "TU", 0)
-            chain("WB", 0, A("WA", 0, 288), "AU0", 0)
+            choose(0, 2, 0, (lambda: chain("ROW0", 288, A("YF", 0, 288), "CU", _U["FU"], "V"),
+                             lambda: scan(A("SR", 288, 576), A("ROW0", 288, 576), 288)))
+            choose(2, 1, 36, (lambda: chain("WA", 0, CF("IOT", 288), "TU", 0),
+                              lambda: value(A("AU0", 18, 36), "SR", 288, 576),
+                              lambda: chain("WB", 0, A("WA", 0, 288), "AU0", 0)))
             chain("WA", 0, A("WB", 0, 288), "TU", 18)
             chain("WB", 0, A("WA", 0, 288), lp, 0)
             chain("WA", 0, A("WB", 0, 288), "TU", 36)
-            chain(yn, 0, A("WA", 0, 288), "AU0", 18)
+            chain("YF", 0, A("WA", 0, 288), "AU0", 18)
+            chain("PP", 0, CF("IOT", 288), lp, 0, False)
+            scan(A("SY", 0, 288), A("YF", 0, 288), 288)
+            value(A("YW", 0, 18), "SY", 0, 288)
+            chain(yn, 0, pp, "YW", 0)
         else:
             msig("V", 2, 0, HALF)
             msig("S", 1, 0, HALF)
@@ -366,12 +375,14 @@ def rank_program(g, core, T, topo):
         scan(A("KC", 0, 144), A("KR", 0, 144), 144)
         gc("V", 0)
         value(A(ks, 0, 9), "KC", 0, 144)
+        for t in (1, 2, 3):
+            gv(t)
+        gc("V", 1)
         send(other, A(kl, 0, 9), A(ks, 0, 9), "ak%d" % r)
         if r == 0:
             cp(CU("FH", 9, 0), A("LI", _L["fd"], _L["fd"] + 9))
             cp(CU("FH", 9, 10), A("LI", _L["fd"] + 9, _L["fd"] + 18))
-        for t in (1, 2, 3):
-            gv(t)
+        for t in (2, 3):
             gc("S", t)
         msig("S", 3, 0, C if r == 0 else HALF)
         rbit("S", 3, LOW)
@@ -429,17 +440,17 @@ def rank_program(g, core, T, topo):
             if r == 0:
                 cp(CU("EXU"), LI("ex"))
                 ts(A("EA", 18, 36), CF("EXF"), 0.25, None, Op.add)
-            scan(A("SR", 0, 288), A(rown, 0, 288), 288)
-            own(2)
-            value(A("AB", 0, 18), "SR", 0, 288)
-            own(3)
-            cp(A(aun, 0, 18), A("AB", 0, 18))
-            send(rank ^ MASK[nr], A("LP%d" % nr, 0, 18), A(aun, 0, 18), "ap%d" % nr)
-            quant(xq, xs, HALF, C, A(xn, 576, 1152))
-            planar(nr, HALF, C)
             chain("YF", 0, A("YG", 0, 288), "CU", _U["FU"], False)
             chain(rown, 288, A("YF", 0, 288), "CU", _U["FU"], False)
+            own(2)
+            own(3)
+            scan(A("SR", 0, 288), A(rown, 0, 288), 288)
+            quant(xq, xs, HALF, C, A(xn, 576, 1152))
+            value(A("AB", 0, 18), "SR", 0, 288)
             scan(A("SR", 288, 576), A(rown, 288, 576), 288)
+            cp(A(aun, 0, 18), A("AB", 0, 18))
+            send(rank ^ MASK[nr], A("LP%d" % nr, 0, 18), A(aun, 0, 18), "ap%d" % nr)
+            planar(nr, HALF, C)
             if r == 0:
                 act(CF("ER", 288), ind(CF("IOT", 288), CU("EXU")))
             act(A("ERO", 0, 288), ind(CF("ER", 288), A(aun, 0, 18)))
@@ -449,9 +460,9 @@ def rank_program(g, core, T, topo):
             for j in (2, 1, 0, 3):
                 mm(j, "uq2", "us2", 128 * j, xq, xs, HALF, C)
                 msig("S", j, HALF, C)
+            if r == 0:
+                quant("EQ", "ES", 0, 512, A("ET", 0, 2048))
             for i, at in ((0, 0), (1, 36)):
-                if r == 0:
-                    quant("EQ", "ES", 256 * i, 256 * i + 256, A("ET", 1024 * i, 1024 * i + 1024))
                 scan(A("SE", 288 * i, 288 * i + 288), A("ERO", 288 * i, 288 * i + 288), 288)
                 value(A("EA", at, at + 18), "SE", 288 * i, 288 * i + 288)
 

from concourse.mybir import dt, AluOpType as Op, ActivationFunctionType as Act

C, HALF = 288, 144
MASK = [4, 1, 2]
K = 65536.0
SLOT = {2: 0, 1: 1, 0: 2, 3: 3}
_F = {}
_n = 0
for _name, _w in (("TM", 288), ("A1", 288), ("A2", 288), ("A0", 288), ("IOT", 288), ("ER", 288), ("FR", 288), ("FF", 288),
                  ("F3", 288), ("F3S", 288), ("KW", 24), ("CW", 24), ("EXF", 24), ("LOWF", 24), ("D1", 24),
                  ("PMF", 8), ("PM1", 8), ("T15", 8), ("INV", 8)):
    _F[_name] = _n
    _n += _w
_L = {"pb": 0, "ex": 24, "fd": 48, "lg": 72, "PI": 96, "PM": 104, "UL": 112}
_U = {"FU": 0, "F3U": 32, "EXU": 64, "LGU": 96, "FH": 160, "ULU": 192}

SCRATCH = {
    "CF": ("sbuf", [128, _n], "float32"), "LI": ("sbuf", [128, 144], "int32"), "CU": ("sbuf", [128, 224], "uint16"),
    "ut": ("sbuf", [128, 512], "bfloat16"), "vt": ("sbuf", [128, 512], "bfloat16"),
    "uq": ("sbuf", [128, 128], "float8_e4m3fn_x4"), "us": ("sbuf", [128, 128], "uint8"),
    "uq2": ("sbuf", [128, 512], "float8_e4m3fn_x4"), "us2": ("sbuf", [128, 512], "uint8"),
    "vq": ("sbuf", [128, 128], "float8_e4m3fn_x4"), "vs": ("sbuf", [128, 128], "uint8"),
    "wq": ("sbuf", [128, 512], "float8_e4m3fn_x4"), "wp": ("sbuf", [128, 512], "uint8"),
    "ONE": ("sbuf", [128, 512], "bfloat16"), "ET": ("sbuf", [128, 2048], "bfloat16"),
    "EQ": ("sbuf", [128, 512], "float8_e4m3fn_x4"), "ES": ("sbuf", [128, 512], "uint8"),
    "A0B": ("sbuf", [128, 576], "bfloat16"),
    "M": ("sbuf", [128, 1152], "bfloat16"), "RB": ("sbuf", [128, 1152], "bfloat16"), "SB": ("sbuf", [128, 1152], "bfloat16"),
    "SR": ("sbuf", [128, 576], "float32"), "ERO": ("sbuf", [128, 576], "float32"), "SE": ("sbuf", [128, 576], "float32"),
    "SY": ("sbuf", [128, 288], "float32"), "PP": ("sbuf", [128, 288], "float32"),
    "WA": ("sbuf", [128, 288], "float32"), "WB": ("sbuf", [128, 288], "float32"),
    "KR": ("sbuf", [128, 304], "float32"), "KC": ("sbuf", [128, 288], "float32"),
    "EA": ("sbuf", [128, 56], "float32"), "DM": ("sbuf", [128, 56], "float32"), "LF": ("sbuf", [128, 56], "float32"),
    "AB": ("sbuf", [128, 56], "float32"), "DP": ("sbuf", [128, 56], "float32"), "LU": ("sbuf", [128, 64], "uint16"),
    "QS": ("sbuf", [128, 144], "float32"), "TU": ("sbuf", [128, 96], "uint16"), "YW": ("sbuf", [128, 32], "uint16"),
    "YG": ("sbuf", [128, 288], "float32"), "YF": ("sbuf", [128, 288], "float32"),
    "PLB": ("sbuf", [128, 576], "float32"), "YO": ("sbuf", [128, 288], "float32"),
    "PS": ("psum", [128, 4096], "float32"),
}
for _r in range(4):
    SCRATCH["X%d" % _r] = ("sbuf", [128, 1152], "bfloat16")
    SCRATCH["XQ%d" % _r] = ("sbuf", [128, 288], "float8_e4m3fn_x4")
    SCRATCH["XS%d" % _r] = ("sbuf", [128, 288], "uint8")
for _r in range(3):
    for _name, _w, _d in (("V", 1152, "bfloat16"), ("VC", 1152, "bfloat16"), ("Z", 1152, "bfloat16"), ("H", 1152, "bfloat16"),
                          ("HP", 576, "bfloat16"), ("XP", 1152, "bfloat16"),
                          ("ZQ", 288, "float8_e4m3fn_x4"), ("ZS", 288, "uint8"), ("HQ", 144, "float8_e4m3fn_x4"),
                          ("HS", 144, "uint8"), ("HL", 144, "float8_e4m3fn_x4"), ("HM", 144, "uint8"),
                          ("KS", 16, "uint16"), ("KL", 16, "uint16"), ("KO", 16, "uint16"), ("LP", 32, "uint16"),
                          ("AU", 64, "uint16"), ("ROW", 576, "float32"), ("YR", 288, "float32")):
        SCRATCH["%s%d" % (_name, _r)] = ("sbuf", [128, _w], _d)

SEMAPHORES = ["cV", "cS", "cT", "cG", "out", "rl"] + ["ld%d" % i for i in range(12)] + \
    ["a%s%d" % (k, r) for k in ("k", "p", "c", "s") for r in range(3)]


def rank_program(g, core, T, topo):
    rank = T.rank_of(core)
    if rank is None:
        return
    eng = {"V": g.vector, "S": g.scalar, "T": g.tensor, "G": g, "Y": g.sync}
    csem = {"V": "cV", "S": "cS", "T": "cT", "G": "cG"}
    count = {"cV": 0, "cS": 0, "cT": 0, "cG": 0, "out": 0, "rl": 0}
    know = {q: {} for q in eng}
    uses = {}
    order = [0]

    def A(name, lo, hi, ph=None):
        ap = T[name][:, lo:hi] if ph is None else T[name][:, lo + ph:hi:4]
        return ap, [(name, lo, hi, ph)]

    def CF(name, w=18, lo=0):
        return A("CF", _F[name] + lo, _F[name] + lo + w)

    def LI(name, w=18):
        return A("LI", _L[name], _L[name] + w)

    def CU(name, w=18, lo=0):
        return A("CU", _U[name] + lo, _U[name] + lo + w)

    def E16(name, lo, hi):
        return T[name][:, lo + 15:hi:16], [(name, lo, hi, None)]

    def B8(name, lo, hi):
        return T[name][:, lo:hi].bitcast(dt.uint8), [(name, lo, hi, None)]

    def ind(win, off):
        return win[0].indirect(off[0]), win[1] + off[1]

    def BANK(i, n):
        return T["PS"][:, 512 * i:512 * i + n], [("PS", i, i + 1, None)]

    def deps(q, ins, outs):
        found = {}
        for regs, w in ((ins, False), (outs, True)):
            for (name, lo, hi, ph) in regs:
                for (l2, h2, p2, w2, op) in uses.get(name, ()):
                    if hi <= l2 or h2 <= lo or not (ph is None or p2 is None or ph == p2):
                        continue
                    same = op["q"] == q and op["compute"]
                    if name == "PS":
                        if same:
                            continue
                    elif not (w or w2) or (same and w and not w2):
                        continue
                    found[op["n"]] = op
        for n in sorted(found, reverse=True):
            op = found[n]
            if know[q].get(op["sem"], 0) < op["val"]:
                eng[q].wait_ge(T.sem[op["sem"]], op["val"])
                know[q][op["sem"]] = op["val"]
                for s, v in op["know"].items():
                    if know[q].get(s, 0) < v:
                        know[q][s] = v

    def note(op, ins, outs):
        order[0] += 1
        op["n"] = order[0]
        for regs, w in ((ins, False), (outs, True)):
            for (name, lo, hi, ph) in regs:
                uses.setdefault(name, []).append((lo, hi, ph, w, op))

    def regs_of(args):
        out = []
        for a in args:
            out += a[1]
        return out

    def emit(q, fn, outs, ins):
        ri, ro = regs_of(ins), regs_of(outs)
        deps(q, ri, ro)
        s = csem[q]
        count[s] += 1
        fn(eng[q]).then_inc(T.sem[s], 1)
        note({"q": q, "compute": True, "sem": s, "val": count[s], "know": dict(know[q])}, ri, ro)

    def load(q, sem, dst, src):
        deps(q, [], dst[1])
        eng[q].dma_start(dst[0], src).then_inc(T.sem[sem], 16)
        note({"q": q, "compute": False, "sem": sem, "val": 16, "know": dict(know[q])}, [], dst[1])

    def store(q, dst, src):
        deps(q, src[1], [])
        eng[q].dma_start(dst, src[0]).then_inc(T.sem.out, 16)
        count["out"] += 16

    def send(to, dst, src, sem):
        c = T.cores[to]
        deps("G", src[1], [])
        rid, pid = topo.addr(c, core)
        n = len(topo.engines(core, c))
        g.remote_dma(dst[0], src[0], T.sem[sem], T.sem.rl, pid, rid, topo.mask(core, c))
        count["rl"] += n
        note({"q": "G", "compute": False, "sem": sem, "val": n, "know": {}}, [], dst[1])

    def sc(a):
        return a[0] if isinstance(a, tuple) else a

    def more(*a):
        return [b for b in a if isinstance(b, tuple)]

    def ts(out, in0, s1, s2, op0, op1=None):
        if op1 is None:
            emit("V", lambda e: e.tensor_scalar(out[0], in0[0], sc(s1), None, op0), [out], [in0] + more(s1))
        else:
            emit("V", lambda e: e.tensor_scalar(out[0], in0[0], sc(s1), sc(s2), op0, op1), [out], [in0] + more(s1, s2))

    def tt(out, a, b, op):
        emit("V", lambda e: e.tensor_tensor(out[0], a[0], b[0], op), [out], [a, b])

    def cp(out, a):
        emit("V", lambda e: e.tensor_copy(out[0], a[0]), [out], [a])

    def act(out, a, f=Act.Copy, scale=1.0):
        emit("S", lambda e: e.activation(out[0], a[0], f, scale=scale), [out], [a])

    def move(q, out, a):
        if q == "V":
            cp(out, a)
        else:
            act(out, a)

    def scan(out, data, n, bits=False):
        d0 = A("A0B", 0, n) if bits else CF("A0", n)
        emit("V", lambda e: e.tensor_tensor_scan(out[0], d0[0], data[0], 0.0, Op.mult, Op.add), [out], [d0, data])

    def quant(qn, sn, lo, hi, src):
        a, b = A(qn, lo, hi), A(sn, lo, hi)
        emit("V", lambda e: e.quantize_mx(a[0], b[0], src[0]), [a, b], [src])

    def mm(bank, wn, sn, wlo, xn, pn, lo, hi):
        o = BANK(bank, hi - lo)
        ins = [A(wn, wlo, wlo + 128), A(sn, wlo, wlo + 128), A(xn, lo, hi), A(pn, lo, hi)]
        emit("T", lambda e: e.matmul_mx(o[0], ins[0][0], ins[1][0], ins[2][0], ins[3][0], True, True), [o], ins)

    def iota(out, pattern, base, mult, f32):
        if f32:
            emit("G", lambda e: e.iota(out[0], pattern, base, mult, allow_small_or_imprecise_dtypes=True), [out], [])
        else:
            emit("G", lambda e: e.iota(out[0], pattern, base, mult), [out], [])

    def planar(r, a, b):
        for t in range(4):
            o, i = A("XP%d" % r, 288 * t + a, 288 * t + b), A("X%d" % r, 4 * a, 4 * b, t)
            emit("G", lambda e: e.affine_select(o[0], i[0], [[0, b - a]], Op.is_gt, 0.0, 1, 0), [o], [i])

    def value(out, sc_name, lo, hi):
        ts(out, E16(sc_name, lo, hi), CF("INV", 1), 0.25, Op.mult, Op.add)

    def chain(out, lo, win, off, o0, split=True):
        if split == "V":
            cp(A(out, lo, lo + 288), ind(win, A(off, o0, o0 + 18)))
        elif split:
            cp(A(out, lo, lo + 160), ind(win, A(off, o0, o0 + 10)))
            act(A(out, lo + 160, lo + 288), ind(win, A(off, o0 + 10, o0 + 18)))
        else:
            act(A(out, lo, lo + 288), ind(win, A(off, o0, o0 + 18)))

    load("Y", "ld0", LI("pb"), T.pb[:, :])
    load("S", "ld1", A("ut", 0, 512), T.u[:, :])
    load("Y", "ld4", A("X0", 0, 1152), T.x[:, :])
    load("S", "ld5", LI("lg"), T.lg[:, :])
    load("S", "ld3", LI("fd"), T.fd[:, :])
    load("Y", "ld2", LI("ex"), T.ex[:, :])
    load("Y", "ld6", B8("wq", 0, 512), T.wc[:, :])
    load("Y", "ld7", A("wp", 0, 512), T.ws[:, :])
    load("Y", "ld8", A("vt", 0, 512), T.v[:, :])

    iota(LI("PI", 1), [[0, 1]], 0, 1, False)
    iota(CF("TM", 288), [[0, 18], [1, 16]], 0, 0, True)
    iota(CF("IOT", 288), [[1, 288]], 0, 0, True)
    iota(LI("UL", 32), [[1, 4], [16, 8]], 0, 0, False)
    iota(CF("KW"), [[16, 18]], 0, 0, True)

    emit("V", lambda e: e.memset(T.ONE[:, :], 1.0), [A("ONE", 0, 512)], [])
    ts(LI("PM", 1), LI("PI", 1), 15, None, Op.bitwise_and)
    cp(CF("PMF", 1), LI("PM", 1))
    ts(CF("PM1", 1), CF("PMF", 1), 1.0, None, Op.add)
    ts(CF("T15", 1), CF("PMF", 1), 15.0, 1.0 - 1.0 / K, Op.is_equal, Op.mult)
    ts(CF("A1", 288), CF("TM", 288), CF("PMF", 1), 1.0, Op.subtract, Op.is_ge)
    ts(CF("A2", 288), CF("TM", 288), CF("PM1", 1), K - 1.0, Op.is_equal, Op.mult)
    ts(CF("INV", 1), CF("T15", 1), 1.0 / K, None, Op.add)
    tt(CF("A0", 288), CF("A1", 288), CF("A2", 288), Op.add)
    cp(A("AU0", 0, 18), LI("pb"))
    send(rank ^ MASK[0], A("LP0", 0, 18), A("AU0", 0, 18), "ap0")
    act(A("A0B", 0, 288), CF("A0", 288))
    act(A("A0B", 288, 576), CF("A0", 288))
    cp(CU("ULU", 32), LI("UL", 32))
    ts(CF("CW"), CF("KW"), CF("PMF", 1), None, Op.add)
    for i in range(3):
        ts(A("AB", 18 * i, 18 * i + 18), CF("CW"), 0.25, None, Op.add)

    planar(0, 0, C)

    def onehot(b):
        emit("G", lambda e: e.affine_select(T.ET[:, 512 * b:512 * b + 512], T.ONE[:, :], [[-1, 512]], Op.is_equal, 0.0, b, 4),
             [A("ET", 512 * b, 512 * b + 512)], [A("ONE", 0, 512)])

    for b in range(4):
        onehot(b)

    cp(CU("LGU"), LI("lg"))
    cp(CU("FU"), LI("fd"))
    chain("YR0", 0, CF("IOT", 288), "CU", _U["LGU"], False)
    def stand(j, n):
        off, o = CU("ULU", 8 * n, 8 * j), (128 * j, 128 * (j + n))
        emit("V", lambda e: e.tensor_copy(T.uq2[:, o[0]:o[1]].bitcast(dt.uint32),
                                          T.uq[:, 0:128].bitcast(dt.uint32).indirect(off[0])),
             [A("uq2", o[0], o[1])], [A("uq", 0, 128), off])
        emit("S", lambda e: e.activation(T.us2[:, o[0]:o[1]], T.us[:, 0:128].indirect(off[0]), Act.Copy),
             [A("us2", o[0], o[1])], [A("us", 0, 128), off])

    cp(CF("EXF"), LI("ex"))
    quant("uq", "us", 0, 128, A("ut", 0, 512))
    tt(CF("LOWF"), CF("EXF"), CF("CW"), Op.min)
    tt(CF("D1"), CF("EXF"), CF("CW"), Op.subtract)
    stand(1, 2)
    cp(A("LU", 18, 36), CF("LOWF"))
    quant("XQ0", "XS0", 0, 288, A("X0", 0, 1152))
    chain("YG", 0, A("YR0", 0, 288), "CU", _U["FU"], False)
    stand(0, 1)
    stand(3, 1)
    for j in (2, 1, 0, 3):
        mm(j, "uq2", "us2", 128 * j, "XQ0", "XS0", 0, 288)
    for i in range(3):
        ts(A("DP", 18 * i, 18 * i + 18), CF("D1"), CF("INV", 1), None, Op.mult)

    def msig(q, j, lo, hi):
        o, i = A("M", 288 * j + lo, 288 * j + hi), BANK(j, hi - lo)
        if q == "V":
            ts(o, i, 0.0, None, Op.is_lt)
        else:
            act(o, i, Act.Sign, -1.0)

    def rbit(q, j, lst):
        s = SLOT[j]
        o, i = A("RB", 288 * s, 288 * s + 288), ind(A("M", 288 * j, 288 * j + 288), lst)
        if q == "V":
            ts(o, i, 0.0, None, Op.max)
        else:
            act(o, i, Act.Relu)

    def choose(s, n, at, between=()):
        a, b = A("QS", 18 * s, 18 * (s + n)), A("QS", 72 + 18 * s, 72 + 18 * (s + n))
        steps = [lambda: scan(A("SB", 288 * s, 288 * (s + n)), A("RB", 288 * s, 288 * (s + n)), 288 * n, bits=True),
                 lambda: tt(a, E16("SB", 288 * s, 288 * (s + n)), A("DP", at, at + 18 * n), Op.mult),
                 lambda: tt(b, a, A("AB", at, at + 18 * n), Op.add),
                 lambda: cp(A("TU", 18 * s, 18 * (s + n)), b)]
        for i, step in enumerate(steps):
            step()
            if i < len(between):
                between[i]()

    LOW = A("LU", 18, 36)

    for r in range(3):
        other = rank ^ MASK[r]
        x, xn, last = "X%d" % r, "X%d" % (r + 1), r == 2
        v, vc, z, h, hp = "V%d" % r, "VC%d" % r, "Z%d" % r, "H%d" % r, "HP%d" % r
        ks, kl, ko, au, lp = "KS%d" % r, "KL%d" % r, "KO%d" % r, "AU%d" % r, "LP%d" % r
        yn = "PLB" if last else "YR%d" % (r + 1)
        yrow = A(yn, 0, 288)
        pp = A("PP", 0, 288)
        if r == 0:
            msig("V", 2, 0, C)
            msig("S", 1, 0, C)
            chain("YF", 0, A("YG", 0, 288), "CU", _U["FU"], "V")
            rbit("V", 2, LOW)
            rbit("S", 1, LOW)
            msig("S", 0, 0, C)
            rbit("S", 0, LOW)
            act(CF("FR", 288), ind(CF("IOT", 288), CU("FU")))
            choose(0, 2, 0, (lambda: chain("ROW0", 288, A("YF", 0, 288), "CU", _U["FU"], "V"),
                             lambda: scan(A("SR", 288, 576), A("ROW0", 288, 576), 288)))
            choose(2, 1, 36, (lambda: chain("WA", 0, CF("IOT", 288), "TU", 0),
                              lambda: value(A("AU0", 18, 36), "SR", 288, 576),
                              lambda: chain("WB", 0, A("WA", 0, 288), "AU0", 0)))
            chain("WA", 0, A("WB", 0, 288), "TU", 18)
            chain("WB", 0, A("WA", 0, 288), lp, 0)
            chain("WA", 0, A("WB", 0, 288), "TU", 36)
            chain("YF", 0, A("WA", 0, 288), "AU0", 18)
            chain("PP", 0, CF("IOT", 288), lp, 0, False)
            scan(A("SY", 0, 288), A("YF", 0, 288), 288)
            value(A("YW", 0, 18), "SY", 0, 288)
            chain(yn, 0, pp, "YW", 0)
        else:
            msig("V", 2, 0, HALF)
            msig("S", 1, 0, HALF)
            rbit("V", 2, A("LU", 0, 18))
            rbit("S", 1, LOW)
            msig("S", 0, 0, HALF)
            chain("PP", 0, CF("IOT", 288), lp, 0, False)
            choose(0, 2, 0)
            rbit("S", 0, A("LU", 36, 54))
            chain("WA", 0, pp, "TU", 0)
            choose(2, 1, 36)
            chain("WB", 0, A("WA", 0, 288), "TU", 18, False)
            chain("WA", 0, A("WB", 0, 288), lp, 0)
            chain(yn, 0, A("WA", 0, 288), "TU", 36)
        scan(A("SY", 0, 288), yrow, 288)
        value(A("YW", 0, 18), "SY", 0, 288)

        def gv(t):
            act(A(v, 288 * t, 288 * t + 288), ind(A("XP%d" % r, 288 * t, 288 * t + 288), A("YW", 0, 18)), Act.Copy, 0.5)

        def gz(t, a, b):
            f = CU("FU") if (a, b) == (0, C) else CU("FH", 9, 10 * (a // HALF))
            w = A(v, 288 * t, 288 * t + 288)
            tt(A(z, 4 * a, 4 * b, t), ind(w, f), A(vc, 288 * t + a, 288 * t + b), Op.add)

        def gc(q, t):
            move(q, A(vc, 288 * t, 288 * t + 288), A(v, 288 * t, 288 * t + 288))

        act(A("KR", 0, 144), ind(CF("FR", 288), A("YW", 0, 9)))
        ts(A(v, 0, 288), ind(A("XP%d" % r, 0, 288), A("YW", 0, 18)), 0.5, None, Op.mult)
        scan(A("KC", 0, 144), A("KR", 0, 144), 144)
        gc("V", 0)
        value(A(ks, 0, 9), "KC", 0, 144)
        for t in (1, 2, 3):
            gv(t)
        gc("V", 1)
        send(other, A(kl, 0, 9), A(ks, 0, 9), "ak%d" % r)
        if r == 0:
            cp(CU("FH", 9, 0), A("LI", _L["fd"], _L["fd"] + 9))
            cp(CU("FH", 9, 10), A("LI", _L["fd"] + 9, _L["fd"] + 18))
        for t in (2, 3):
            gc("S", t)
        msig("S", 3, 0, C if r == 0 else HALF)
        rbit("S", 3, LOW)
        act(A("KR", 144, 304), ind(CF("FR", 288), A("YW", 8, 18)))
        zq, zs = "ZQ%d" % r, "ZS%d" % r
        for t in (0, 1, 2):
            gz(t, 0, C)
        gz(3, 0, HALF)
        quant(zq, zs, 0, HALF, A(z, 0, 576))
        gz(3, HALF, C)
        quant(zq, zs, HALF, C, A(z, 576, 1152))

        def ev(q, hf, b):
            o, i = A(h, 288 * b + 144 * hf, 288 * b + 144 * hf + 144), BANK(4 * hf + b, HALF)
            if q == "V":
                ts(o, i, 0.03125, None, Op.mult)
            else:
                act(o, i, Act.Copy, 0.03125)

        for b in range(4):
            mm(b, "wq", "wp", 128 * b, zq, zs, 0, HALF)
            ev("S", 0, b)
        for b in range(4):
            mm(4 + b, "wq", "wp", 128 * b, zq, zs, HALF, C)
            ev("S" if b < 2 else "V", 1, b)
        for q, b, at, to in (("S", 0, 0, 9), ("V", 2, 0, 9), ("S", 1, 0, 9), ("V", 3, 0, 4), ("S", 3, 4, 9)):
            move(q, A(hp, 64 * at, 64 * to, b), ind(A(h, 288 * b, 288 * b + 288), A(kl, at, to)))
        hq, hs, hl, hm = "HQ%d" % r, "HS%d" % r, "HL%d" % r, "HM%d" % r
        quant(hq, hs, 0, HALF, A(hp, 0, 576))
        send(other, B8(hl, 0, HALF), B8(hq, 0, HALF), "ac%d" % r)
        send(other, A(hm, 0, HALF), A(hs, 0, HALF), "as%d" % r)
        def own(b):
            tt(A(xn, 576, 1152, b), ind(A(h, 288 * b, 288 * b + 288), A(ko, 0, 9)), A(x, 576, 1152, b), Op.add)

        nr = r + 1
        xq, xs = "XQ%d" % nr, "XS%d" % nr
        rown, aun = ("PLB" if last else "ROW%d" % nr), "AU%d" % nr
        plo = 288 if last else 0
        prow_old = A("ROW%d" % r, 0, 288)
        if r == 0:
            act(prow_old, ind(CF("IOT", 288), A("AU0", 0, 18)))
        if not last:
            chain("YG", 0, yrow, "CU", _U["FU"], False)
        choose(3, 1, 18, (lambda: scan(A("KC", 144, 288), A("KR", 160, 304), 144),
                          lambda: value(A(ko, 0, 9), "KC", 144, 288), lambda: own(0)))
        act(A(rown, plo, plo + 288), ind(prow_old, A("TU", 54, 72)))
        if last:
            store("Y", T.pl[:, :], (T.PLB[0:128:16, :], [("PLB", 0, 576, None)]))
            for b in (1, 2, 3):
                own(b)
            quant(xq, xs, HALF, C, A(xn, 576, 1152))
            quant("vq", "vs", 0, 128, A("vt", 0, 512))
        else:
            own(1)
            if r == 0:
                cp(CU("EXU"), LI("ex"))
                ts(A("EA", 18, 36), CF("EXF"), 0.25, None, Op.add)
            chain("YF", 0, A("YG", 0, 288), "CU", _U["FU"], False)
            chain(rown, 288, A("YF", 0, 288), "CU", _U["FU"], False)
            own(2)
            own(3)
            scan(A("SR", 0, 288), A(rown, 0, 288), 288)
            quant(xq, xs, HALF, C, A(xn, 576, 1152))
            value(A("AB", 0, 18), "SR", 0, 288)
            scan(A("SR", 288, 576), A(rown, 288, 576), 288)
            cp(A(aun, 0, 18), A("AB", 0, 18))
            send(rank ^ MASK[nr], A("LP%d" % nr, 0, 18), A(aun, 0, 18), "ap%d" % nr)
            planar(nr, HALF, C)
            if r == 0:
                act(CF("ER", 288), ind(CF("IOT", 288), CU("EXU")))
            act(A("ERO", 0, 288), ind(CF("ER", 288), A(aun, 0, 18)))
            value(A("AB", 36, 54), "SR", 288, 576)
            cp(A(aun, 18, 36), A("AB", 36, 54))
            act(A("ERO", 288, 576), ind(CF("ER", 288), A(aun, 18, 36)))
            for j in (2, 1, 0, 3):
                mm(j, "uq2", "us2", 128 * j, xq, xs, HALF, C)
                msig("S", j, HALF, C)
            if r == 0:
                quant("EQ", "ES", 0, 512, A("ET", 0, 2048))
            for i, at in ((0, 0), (1, 36)):
                scan(A("SE", 288 * i, 288 * i + 288), A("ERO", 288 * i, 288 * i + 288), 288)
                value(A("EA", at, at + 18), "SE", 288 * i, 288 * i + 288)

        def yout(a, b, bank):
            mm(bank, "vq", "vs", 0, xq, xs, a, b)
            act(A("YO", a, b), BANK(bank, b - a))

        def osc(q, k, a, b):
            store(q, T.osc[4 * k:4 * k + 4, a:b], (T[xs][32 * k:32 * k + 4, a:b], [(xs, a, b, None)]))

        def stores(a, b):
            yout(a, b, a // HALF)
            store("Y", T.oc[:, 4 * a:4 * b], B8(xq, a, b))
            store("S", T.y[:, a:b], A("YO", a, b))
            for k in range(4):
                osc("Y" if k < 3 else "S", k, a, b)

        if last:
            stores(HALF, C)
        for b in range(4):
            mm(4 + b, "EQ", "ES", 128 * b, hl, hm, 0, HALF)
            tt(A(xn, 0, 576, b), A(x, 0, 576, b), BANK(4 + b, HALF), Op.add)
        quant(xq, xs, 0, HALF, A(xn, 0, 576))
        if last:
            stores(0, HALF)
        else:
            planar(nr, 0, HALF)
            tt(A("LF", 0, 54), A("EA", 0, 54), A("AB", 0, 54), Op.min)
            tt(A("DM", 0, 54), A("EA", 0, 54), A("AB", 0, 54), Op.subtract)
            cp(A("LU", 0, 54), A("LF", 0, 54))
            ts(A("DP", 0, 54), A("DM", 0, 54), CF("INV", 1), None, Op.mult)
            for j in (2, 1, 0, 3):
                mm(j, "uq2", "us2", 128 * j, xq, xs, 0, HALF)
    for s in ("cV", "cS", "cT", "cG", "out", "rl"):
        g.wait_ge(T.sem[s], count[s])
